import numpy as np
import ml_dtypes


def mxq(x, axis, fmt="e4m3"):
    dtype, down = {"e4m3": (ml_dtypes.float8_e4m3fn, 7), "e5m2": (ml_dtypes.float8_e5m2, 14)}[fmt]
    v = np.moveaxis(np.asarray(x, np.float32).astype(ml_dtypes.bfloat16).astype(np.float64), axis, -1)
    blocks = v.reshape(v.shape[:-1] + (-1, 32))
    amax = np.abs(blocks).max(-1, keepdims=True)
    byte = np.maximum(np.where(amax > 0, np.frexp(amax)[1] - 1 + 127, 0) - down, 1)
    scale = np.exp2(byte - 127.0)
    codes = (blocks / scale).astype(np.float32).astype(dtype).astype(np.float64)
    return np.moveaxis((codes * scale).reshape(v.shape), -1, axis)


WIDE = False


def mx_kscale(k):
    if not WIDE:
        return np.ones(k)
    levels = np.array([10, -10, 5, -5, 0])
    if k % 512:
        return np.exp2(np.random.permutation(np.resize(levels, k // 32))).repeat(32)
    a = np.empty((k // 512, 16))
    for p in range(k // 512):
        a[p, :8] = np.random.permutation(np.resize(levels, 8))
        for g in range(8):
            far = levels[np.abs(levels - a[p, g]) >= 10]
            a[p, g + 8] = far[np.random.randint(len(far))]
    return np.exp2(a.ravel()).repeat(32)


def f64(x):
    return np.asarray(x).astype(np.float64)


def striped(idx):
    return np.tile(np.asarray(idx).reshape(-1, 16).T, (8, 1)).astype(np.uint16)


def unstriped(offs):
    return offs[:16].T.reshape(-1).astype(np.int64)


E2M1 = np.array([0.0, 0.5, 1.0, 1.5, 2.0, 3.0, 4.0, 6.0, -0.0, -0.5, -1.0, -1.5, -2.0, -3.0, -4.0, -6.0])


def pack_weight(w, fmt):
    k, n = w.shape
    w = f64(np.asarray(w, np.float32).astype(ml_dtypes.bfloat16)).reshape(k // 32, 32, n)
    amax = np.abs(w).max(1)
    if fmt == "e4m3":
        byte = np.frexp(amax)[1] - 1 + 127 - 7
    else:
        mant, ex = np.frexp(amax / 6.0)
        byte = np.where(mant > 0.5, ex, ex - 1) + 127
    byte = np.clip(np.where(amax > 0, byte, 1), 1, 254)
    scaled = (w * np.exp2(127.0 - byte)[:, None, :]).reshape(k, n).astype(np.float32)
    by_word = np.ascontiguousarray(scaled.reshape(k // 512, 128, 4, n).transpose(0, 1, 3, 2))
    if fmt == "e4m3":
        words = by_word.astype(ml_dtypes.float8_e4m3fn).view(np.uint8)
    else:
        c = by_word.astype(ml_dtypes.float4_e2m1fn).view(np.uint8) & 0xF
        words = (c[..., 0::2] | (c[..., 1::2] << 4)).reshape(k // 512, 128, 2 * n)
    return np.ascontiguousarray(words), np.ascontiguousarray(byte.astype(np.uint8).reshape(k // 512, 16, n))


def unpack_weight(words, scales, fmt):
    g, _, n = scales.shape
    words = np.ascontiguousarray(words).reshape(g, 128, n, -1)
    if fmt == "e4m3":
        vals = words.view(ml_dtypes.float8_e4m3fn).astype(np.float64)
    else:
        nib = np.empty((g, 128, n, 4), np.uint8)
        nib[..., 0::2] = words & 0xF
        nib[..., 1::2] = words >> 4
        vals = E2M1[nib]
    vals = vals * np.repeat(np.exp2(scales.astype(np.float64) - 127.0), 8, axis=1)[..., None]
    return vals.transpose(0, 1, 3, 2).reshape(g * 512, n)


def softplus(v):
    return np.log(1.0 + np.exp(v))


B, N, T, D, NQ = 1, 512, 2048, 1024, 256


def setup_inputs():
    n = np.random.standard_normal
    idx = np.random.permutation(T)[:B * N]
    s = mx_kscale(D)[:, None]
    kp = pack_weight(n((D, T)) / s, "e2m1")
    return {
        "qT": (n((B, D, NQ)) * s * (1.00 / np.sqrt(D))).astype(np.float32),
        "k_words": np.ascontiguousarray(kp[0].reshape(1, 2, 128, T, 2).transpose(0, 2, 3, 1, 4)).reshape(1, 128, T, 4),
        "k_scales": kp[1],
        "ib": np.tile(0.5 * n(2048), (128, 1)).astype(np.float32),
        "ps": (n((B, NQ, 1)) + 1).astype(np.float32),
        "offs": striped(idx),
    }


def reference(qT, k_words, k_scales, ib, ps, offs):
    idx = unstriped(offs)
    pick = lambda x, which: x[:, which].reshape(x.shape[0], B, -1).transpose(1, 0, 2)
    k = unpack_weight(k_words.reshape(1, 128, T, 2, 2).transpose(0, 3, 1, 2, 4).reshape(2, 128, 2 * T), k_scales, "e2m1")
    kg = pick(k, idx)
    qq = mxq(f64(qT), 1, "e4m3")
    a = qq.transpose(0, 2, 1) @ kg
    y = softplus(a + pick(f64(ib), idx)[:, :1, :] - f64(ps))
    return y

@@ -1,0 +1,155 @@
+from contextlib import ExitStack
+
+import concourse.mybir as mybir
+from concourse.masks import make_identity
+
+N, T, D, NQ = 512, 2048, 1024, 256
+FLOPS = 2 * D * NQ * N
+
+F32 = mybir.dt.float32
+BF16 = mybir.dt.bfloat16
+I32 = mybir.dt.int32
+U32 = mybir.dt.uint32
+U16 = mybir.dt.uint16
+U8 = mybir.dt.uint8
+FP8X4 = mybir.dt.float8_e4m3fn_x4
+FP4X4 = mybir.dt.float4_e2m1fn_x4
+ALU = mybir.AluOpType
+ACT = mybir.ActivationFunctionType
+
+P = 128
+PACK = 4
+PASSES = D // (P * PACK)
+Q_TILES = NQ // P
+BIAS_ROW = 8
+CHUNK = 256
+EXP_CAP = 2.0 ** 60
+
+
+def tile_attend_bpr_topk_kernel(tc, qT, k_words, k_scales, ib, ps, offs, out):
+    nc = tc.nc
+    with ExitStack() as ctx:
+        keep = ctx.enter_context(tc.tile_pool(name="keep", bufs=1))
+        psum = ctx.enter_context(tc.psum_pool(name="psum", bufs=1))
+
+        offsets = keep.tile([P, N // 16], U16, name="offsets")
+        nc.sync.dma_start(offsets[:], offs)
+
+        scale_pool = keep.tile([P, PASSES, T], U8, name="scale_pool", align_bytes=64)
+        nc.vector.memset(scale_pool[:].rearrange("p o t -> p (o t)").bitcast(I32), 0)
+        for quad in range(4):
+            nc.scalar.dma_start(
+                out=scale_pool[32 * quad : 32 * quad + 4, :, :].bitcast(I32),
+                in_=k_scales[:, 4 * quad : 4 * quad + 4, :].rearrange("o f t -> f o t").bitcast(I32),
+            )
+
+        word_pool = keep.tile([P, T], U32, name="word_pool", align_bytes=64)
+        nc.sync.dma_start(
+            out=word_pool[:].bitcast(I32),
+            in_=k_words[0].rearrange("p t b -> p (t b)").bitcast(I32),
+        )
+        q_raw = []
+        for o in range(PASSES):
+            raw = keep.tile([P, PACK, NQ], F32, name="q_raw%d" % o, align_bytes=64)
+            nc.sync.dma_start(
+                out=raw[:],
+                in_=qT[0, o * P * PACK : (o + 1) * P * PACK, :].rearrange("(p j) n -> p j n", j=PACK),
+            )
+            q_raw.append(raw)
+
+        zero = keep.tile([P, 1], F32, name="zero")
+        nc.vector.memset(zero[:], 0.0)
+        one = keep.tile([P, 1], F32, name="one")
+        nc.scalar.activation(out=one[:], in_=zero[:], func=ACT.Exp)
+        bias_pool = keep.tile([P, T], F32, name="bias_pool", align_bytes=64)
+        nc.vector.memset(bias_pool[:], 0.0)
+
+        ident = keep.tile([P, P], F32, name="ident", align_bytes=64)
+        make_identity(nc, ident[:])
+        pos = keep.tile([P, Q_TILES], F32, name="pos")
+        with nc.allow_non_contiguous_dma(reason="one positive score a partition and query tile"):
+            nc.gpsimd.dma_start(out=pos[:], in_=ps[0].rearrange("(m p) one -> p (m one)", p=P))
+        nc.gpsimd.dma_start(out=bias_pool[BIAS_ROW : BIAS_ROW + 1, :], in_=ib[0:1, :])
+
+        k_scale = [keep.tile([P, N], U8, name="k_scale%d" % o, align_bytes=64) for o in range(PASSES)]
+        k_code = [keep.tile([P, 2 * N], U8, name="k_code%d" % o, align_bytes=64) for o in range(PASSES)]
+        word_pairs = keep.tile([P, N], U32, name="word_pairs", align_bytes=64)
+        halves = word_pairs[:].bitcast(U16).rearrange("p (n o) -> p o n", o=PASSES)
+
+        nc.vector.tensor_copy(k_scale[0][:], scale_pool[:, 0, :].indirect(offsets[:]))
+        nc.vector.tensor_copy(word_pairs[:], word_pool[:].indirect(offsets[:]))
+        nc.vector.tensor_copy(k_scale[1][:], scale_pool[:, 1, :].indirect(offsets[:]))
+        for o in range(PASSES):
+            nc.vector.tensor_copy(k_code[o][:].bitcast(U16), halves[:, o, :])
+
+        bias_row = keep.tile([P, N], F32, name="bias_row", align_bytes=64)
+        nc.vector.tensor_copy(bias_row[:], bias_pool[:].indirect(offsets[:]))
+
+        blocks = N // P
+        turned = psum.tile([P, blocks, P], F32, name="turned")
+        for c in range(blocks):
+            nc.tensor.transpose(turned[:, c, :], bias_row[:, c * P : (c + 1) * P], ident[:])
+        bias_col = keep.tile([P, blocks], F32, name="bias_col")
+        nc.scalar.copy(out=bias_col[:], in_=turned[:, :, BIAS_ROW])
+        spread = psum.tile([P, N], F32, name="spread")
+        for c in range(blocks):
+            nc.tensor.transpose(
+                spread[:, c * P : (c + 1) * P], bias_col[:, c : c + 1].to_broadcast([P, P]), ident[:]
+            )
+        bias_all = keep.tile([P, N], F32, name="bias_all", align_bytes=64)
+        nc.scalar.copy(out=bias_all[:], in_=spread[:])
+
+        q_code = {}
+        q_scale = {}
+        grouped = {}
+        for o in range(PASSES):
+            for m in range(Q_TILES):
+                g = keep.tile([P, P, PACK], BF16, name="grouped%d%d" % (o, m), align_bytes=64)
+                src = q_raw[o][:, :, m * P : (m + 1) * P].rearrange("p j (c i) -> p c j i", i=4)
+                dst = g[:].rearrange("p (c i) j -> p c j i", i=4)
+                if (o, m) == (1, 0):
+                    nc.vector.tensor_copy(out=dst, in_=src)
+                else:
+                    nc.scalar.copy(out=dst, in_=src)
+                grouped[o, m] = g
+        for o in range(PASSES):
+            for m in range(Q_TILES):
+                q_code[o, m] = keep.tile([P, P], U32, name="q_code%d%d" % (o, m), align_bytes=64)
+                q_scale[o, m] = keep.tile([P, P], U8, name="q_scale%d%d" % (o, m), align_bytes=64)
+                nc.vector.quantize_mx(
+                    out=q_code[o, m][:].bitcast(FP8X4),
+                    scales=q_scale[o, m][:],
+                    in_=grouped[o, m][:].rearrange("p n j -> p (n j)"),
+                )
+
+        acc = [psum.tile([P, N], F32, name="acc%d" % m) for m in range(Q_TILES)]
+        for o in range(PASSES):
+            for m in range(Q_TILES):
+                nc.tensor.matmul_mx(
+                    out=acc[m][:],
+                    lhsT=q_code[o, m][:].bitcast(FP8X4),
+                    lhsT_scale=q_scale[o, m][:],
+                    rhs=k_code[o][:].bitcast(FP4X4),
+                    rhs_scale=k_scale[o][:],
+                    start=(o == 0),
+                    stop=(o == PASSES - 1),
+                )
+
+        chunks = [(m, slice(c, c + CHUNK)) for m in range(Q_TILES) for c in range(0, N, CHUNK)]
+        logit = [keep.tile([P, CHUNK], F32, name="logit%d" % u) for u in range(len(chunks))]
+        grown = [keep.tile([P, CHUNK], F32, name="grown%d" % u) for u in range(len(chunks))]
+        capped = [keep.tile([P, CHUNK], F32, name="capped%d" % u) for u in range(len(chunks))]
+        logged = [keep.tile([P, CHUNK], F32, name="logged%d" % u) for u in range(len(chunks))]
+        result = [keep.tile([P, CHUNK], F32, name="result%d" % u) for u in range(len(chunks))]
+        for u, (m, cols) in enumerate(chunks):
+            nc.vector.scalar_tensor_tensor(
+                out=logit[u][:], in0=acc[m][:, cols], scalar=pos[:, m : m + 1], in1=bias_all[:, cols],
+                op0=ALU.subtract, op1=ALU.add,
+            )
+            nc.scalar.activation(out=grown[u][:], in_=logit[u][:], func=ACT.Exp)
+        for u in range(len(chunks)):
+            nc.vector.tensor_scalar_min(out=capped[u][:], in0=grown[u][:], scalar1=EXP_CAP)
+        for u, (m, cols) in enumerate(chunks):
+            nc.scalar.activation(out=logged[u][:], in_=capped[u][:], func=ACT.Ln, bias=one[:])
+            nc.vector.tensor_tensor(out=result[u][:], in0=logged[u][:], in1=logit[u][:], op=ALU.max)
+            nc.sync.dma_start(out=out[0, m * P : (m + 1) * P, cols], in_=result[u][:])

@@ -21,8 +21,8 @@ P = 128
 PACK = 4
 PASSES = D // (P * PACK)
 Q_TILES = NQ // P
-BIAS_ROW = 8
 CHUNK = 256
+EARLY = 512
 EXP_CAP = 2.0 ** 60
 
 
@@ -34,101 +34,91 @@ def tile_attend_bpr_topk_kernel(tc, qT, k_words, k_scales, ib, ps, offs, out):
 
         offsets = keep.tile([P, N // 16], U16, name="offsets")
         nc.sync.dma_start(offsets[:], offs)
-
-        scale_pool = keep.tile([P, PASSES, T], U8, name="scale_pool", align_bytes=64)
-        nc.vector.memset(scale_pool[:].rearrange("p o t -> p (o t)").bitcast(I32), 0)
-        for quad in range(4):
-            nc.scalar.dma_start(
-                out=scale_pool[32 * quad : 32 * quad + 4, :, :].bitcast(I32),
-                in_=k_scales[:, 4 * quad : 4 * quad + 4, :].rearrange("o f t -> f o t").bitcast(I32),
-            )
+        bias_in = keep.tile([P, T // P], F32, name="bias_in", tag="chain0", align_bytes=64)
+        nc.sync.dma_start(out=bias_in[:], in_=ib[0].rearrange("(p c) -> p c", p=P))
 
         word_pool = keep.tile([P, T], U32, name="word_pool", align_bytes=64)
-        nc.sync.dma_start(
-            out=word_pool[:].bitcast(I32),
-            in_=k_words[0].rearrange("p t b -> p (t b)").bitcast(I32),
-        )
-        q_raw = []
+        word_rows = k_words[0].rearrange("p t b -> p (t b)").bitcast(I32)
+        nc.sync.dma_start(out=word_pool[:, :EARLY].bitcast(I32), in_=word_rows[:, :EARLY])
+
+        scale_pool = keep.tile([P, T], U8, name="scale_pool", align_bytes=64)
+        nc.vector.memset(scale_pool[:].bitcast(I32), 0)
+        scale_rows = k_scales.bitcast(I32).rearrange("o (quad r) t -> r quad o t", r=4)
+        for r in range(4):
+            nc.sync.dma_start(out=scale_pool[r:P:16, :].bitcast(I32), in_=scale_rows[r])
+
+        q_raw = [keep.tile([P, PACK, NQ], F32, name="q_raw%d" % o, align_bytes=64) for o in range(PASSES)]
+        q_rows = qT[0].rearrange("(o p j) n -> o p j n", p=P, j=PACK)
+        nc.sync.dma_start(out=word_pool[:, EARLY:].bitcast(I32), in_=word_rows[:, EARLY:])
         for o in range(PASSES):
-            raw = keep.tile([P, PACK, NQ], F32, name="q_raw%d" % o, align_bytes=64)
-            nc.sync.dma_start(
-                out=raw[:],
-                in_=qT[0, o * P * PACK : (o + 1) * P * PACK, :].rearrange("(p j) n -> p j n", j=PACK),
-            )
-            q_raw.append(raw)
-
-        zero = keep.tile([P, 1], F32, name="zero")
-        nc.vector.memset(zero[:], 0.0)
-        one = keep.tile([P, 1], F32, name="one")
-        nc.scalar.activation(out=one[:], in_=zero[:], func=ACT.Exp)
-        bias_pool = keep.tile([P, T], F32, name="bias_pool", align_bytes=64)
-        nc.vector.memset(bias_pool[:], 0.0)
-
-        ident = keep.tile([P, P], F32, name="ident", align_bytes=64)
-        make_identity(nc, ident[:])
+            nc.sync.dma_start(out=q_raw[o][:], in_=q_rows[o])
         pos = keep.tile([P, Q_TILES], F32, name="pos")
         with nc.allow_non_contiguous_dma(reason="one positive score a partition and query tile"):
-            nc.gpsimd.dma_start(out=pos[:], in_=ps[0].rearrange("(m p) one -> p (m one)", p=P))
-        nc.gpsimd.dma_start(out=bias_pool[BIAS_ROW : BIAS_ROW + 1, :], in_=ib[0:1, :])
+            nc.sync.dma_start(out=pos[:], in_=ps[0].rearrange("(m p) one -> p (m one)", p=P))
+
+        ident = keep.tile([P, P], F32, name="ident", tag="chain1", align_bytes=64)
+        make_identity(nc, ident[:])
+
+        bias_pool = keep.tile([P, T], F32, name="bias_pool", align_bytes=64)
+        bias_runs = bias_pool[:].rearrange("p (j b i) -> p b j i", b=4, i=4)
+        for b in range(4):
+            spread = psum.tile([P, 4, P], F32, name="spread%d" % b)
+            for i in range(4):
+                c = 4 * b + i
+                nc.tensor.transpose(spread[:, i, :], bias_in[:, c : c + 1].to_broadcast([P, P]), ident[:])
+            nc.scalar.copy(out=bias_runs[:, b], in_=spread[:].rearrange("p i j -> p j i"))
 
         k_scale = [keep.tile([P, N], U8, name="k_scale%d" % o, align_bytes=64) for o in range(PASSES)]
         k_code = [keep.tile([P, 2 * N], U8, name="k_code%d" % o, align_bytes=64) for o in range(PASSES)]
-        word_pairs = keep.tile([P, N], U32, name="word_pairs", align_bytes=64)
-        halves = word_pairs[:].bitcast(U16).rearrange("p (n o) -> p o n", o=PASSES)
+        nc.vector.memset(k_scale[1][:].bitcast(I32), 0)
+        nc.vector.tensor_copy(k_scale[0][:], scale_pool[:].indirect(offsets[:]))
+        nc.sync.dma_start(out=k_scale[1][0 : P - 16, :].bitcast(I32), in_=k_scale[0][16:P, :].bitcast(I32))
 
-        nc.vector.tensor_copy(k_scale[0][:], scale_pool[:, 0, :].indirect(offsets[:]))
+        grouped = [
+            keep.tile([P, NQ, PACK], BF16, name="grouped%d" % o, tag="chain%d" % o, align_bytes=64)
+            for o in range(PASSES)
+        ]
+        q_scale = [keep.tile([P, NQ], U8, name="q_scale%d" % o, align_bytes=64) for o in range(PASSES)]
+
+        def interleave(o, m):
+            rows = slice(m * P, (m + 1) * P)
+            nc.scalar.copy(
+                out=grouped[o][:, rows, :].rearrange("p (c i) j -> p c j i", i=4),
+                in_=q_raw[o][:, :, rows].rearrange("p j (c i) -> p c j i", i=4),
+            )
+
+        def quantise(o, rows):
+            nc.vector.quantize_mx(
+                out=q_code[:, o, rows].bitcast(FP8X4),
+                scales=q_scale[o][:, rows],
+                in_=grouped[o][:, rows, :].rearrange("p n j -> p (n j)"),
+            )
+
+        for o in range(PASSES):
+            for m in range(Q_TILES):
+                interleave(o, m)
+
+        word_pairs = keep.tile([P, N], U32, name="word_pairs", tag="words", align_bytes=64)
+        halves = word_pairs[:].bitcast(U16).rearrange("p (n o) -> p o n", o=PASSES)
         nc.vector.tensor_copy(word_pairs[:], word_pool[:].indirect(offsets[:]))
-        nc.vector.tensor_copy(k_scale[1][:], scale_pool[:, 1, :].indirect(offsets[:]))
         for o in range(PASSES):
             nc.vector.tensor_copy(k_code[o][:].bitcast(U16), halves[:, o, :])
-
-        bias_row = keep.tile([P, N], F32, name="bias_row", align_bytes=64)
-        nc.vector.tensor_copy(bias_row[:], bias_pool[:].indirect(offsets[:]))
-
-        blocks = N // P
-        turned = psum.tile([P, blocks, P], F32, name="turned")
-        for c in range(blocks):
-            nc.tensor.transpose(turned[:, c, :], bias_row[:, c * P : (c + 1) * P], ident[:])
-        bias_col = keep.tile([P, blocks], F32, name="bias_col")
-        nc.scalar.copy(out=bias_col[:], in_=turned[:, :, BIAS_ROW])
-        spread = psum.tile([P, N], F32, name="spread")
-        for c in range(blocks):
-            nc.tensor.transpose(
-                spread[:, c * P : (c + 1) * P], bias_col[:, c : c + 1].to_broadcast([P, P]), ident[:]
-            )
-        bias_all = keep.tile([P, N], F32, name="bias_all", align_bytes=64)
-        nc.scalar.copy(out=bias_all[:], in_=spread[:])
-
-        q_code = {}
-        q_scale = {}
-        grouped = {}
+        q_code = keep.tile([P, PASSES, NQ], U32, name="q_code", tag="words", align_bytes=64)
+        bias = []
         for o in range(PASSES):
             for m in range(Q_TILES):
-                g = keep.tile([P, P, PACK], BF16, name="grouped%d%d" % (o, m), align_bytes=64)
-                src = q_raw[o][:, :, m * P : (m + 1) * P].rearrange("p j (c i) -> p c j i", i=4)
-                dst = g[:].rearrange("p (c i) j -> p c j i", i=4)
-                if (o, m) == (1, 0):
-                    nc.vector.tensor_copy(out=dst, in_=src)
-                else:
-                    nc.scalar.copy(out=dst, in_=src)
-                grouped[o, m] = g
-        for o in range(PASSES):
-            for m in range(Q_TILES):
-                q_code[o, m] = keep.tile([P, P], U32, name="q_code%d%d" % (o, m), align_bytes=64)
-                q_scale[o, m] = keep.tile([P, P], U8, name="q_scale%d%d" % (o, m), align_bytes=64)
-                nc.vector.quantize_mx(
-                    out=q_code[o, m][:].bitcast(FP8X4),
-                    scales=q_scale[o, m][:],
-                    in_=grouped[o, m][:].rearrange("p n j -> p (n j)"),
-                )
+                quantise(o, slice(m * P, (m + 1) * P))
+            half = keep.tile([P, CHUNK], F32, name="bias%d" % o, tag="chain%d" % o, align_bytes=64)
+            nc.vector.tensor_copy(half[:], bias_pool[:].indirect(offsets[:, o * 16 : (o + 1) * 16]))
+            bias.append(half)
 
         acc = [psum.tile([P, N], F32, name="acc%d" % m) for m in range(Q_TILES)]
         for o in range(PASSES):
             for m in range(Q_TILES):
                 nc.tensor.matmul_mx(
                     out=acc[m][:],
-                    lhsT=q_code[o, m][:].bitcast(FP8X4),
-                    lhsT_scale=q_scale[o, m][:],
+                    lhsT=q_code[:, o, m * P : (m + 1) * P].bitcast(FP8X4),
+                    lhsT_scale=q_scale[o][:, m * P : (m + 1) * P],
                     rhs=k_code[o][:].bitcast(FP4X4),
                     rhs_scale=k_scale[o][:],
                     start=(o == 0),
@@ -137,19 +127,18 @@ def tile_attend_bpr_topk_kernel(tc, qT, k_words, k_scales, ib, ps, offs, out):
 
         chunks = [(m, slice(c, c + CHUNK)) for m in range(Q_TILES) for c in range(0, N, CHUNK)]
         logit = [keep.tile([P, CHUNK], F32, name="logit%d" % u) for u in range(len(chunks))]
-        grown = [keep.tile([P, CHUNK], F32, name="grown%d" % u) for u in range(len(chunks))]
-        capped = [keep.tile([P, CHUNK], F32, name="capped%d" % u) for u in range(len(chunks))]
+        grown = keep.tile([P, len(chunks), CHUNK], F32, name="grown")
+        capped = keep.tile([P, len(chunks), CHUNK], F32, name="capped")
         logged = [keep.tile([P, CHUNK], F32, name="logged%d" % u) for u in range(len(chunks))]
         result = [keep.tile([P, CHUNK], F32, name="result%d" % u) for u in range(len(chunks))]
         for u, (m, cols) in enumerate(chunks):
             nc.vector.scalar_tensor_tensor(
-                out=logit[u][:], in0=acc[m][:, cols], scalar=pos[:, m : m + 1], in1=bias_all[:, cols],
+                out=logit[u][:], in0=acc[m][:, cols], scalar=pos[:, m : m + 1], in1=bias[u % 2][:],
                 op0=ALU.subtract, op1=ALU.add,
             )
-            nc.scalar.activation(out=grown[u][:], in_=logit[u][:], func=ACT.Exp)
-        for u in range(len(chunks)):
-            nc.vector.tensor_scalar_min(out=capped[u][:], in0=grown[u][:], scalar1=EXP_CAP)
+            nc.scalar.activation(out=grown[:, u, :], in_=logit[u][:], func=ACT.Exp)
+        nc.vector.tensor_scalar_min(out=capped[:], in0=grown[:], scalar1=EXP_CAP)
         for u, (m, cols) in enumerate(chunks):
-            nc.scalar.activation(out=logged[u][:], in_=capped[u][:], func=ACT.Ln, bias=one[:])
+            nc.scalar.activation(out=logged[u][:], in_=capped[:, u, :], func=ACT.Ln, bias=1.0)
             nc.vector.tensor_tensor(out=result[u][:], in0=logged[u][:], in1=logit[u][:], op=ALU.max)
             nc.sync.dma_start(out=out[0, m * P : (m + 1) * P, cols], in_=result[u][:])

@@ -41,7 +41,7 @@ def tile_attend_bpr_topk_kernel(tc, qT, k_words, k_scales, ib, ps, offs, out):
         word_rows = k_words[0].rearrange("p t b -> p (t b)").bitcast(I32)
         nc.sync.dma_start(out=word_pool[:, :EARLY].bitcast(I32), in_=word_rows[:, :EARLY])
 
-        scale_pool = keep.tile([P, T], U8, name="scale_pool", align_bytes=64)
+        scale_pool = keep.tile([P, T], U8, name="scale_pool", tag="scales", align_bytes=64)
         nc.vector.memset(scale_pool[:].bitcast(I32), 0)
         scale_rows = k_scales.bitcast(I32).rearrange("o (quad r) t -> r quad o t", r=4)
         for r in range(4):
@@ -52,9 +52,6 @@ def tile_attend_bpr_topk_kernel(tc, qT, k_words, k_scales, ib, ps, offs, out):
         nc.sync.dma_start(out=word_pool[:, EARLY:].bitcast(I32), in_=word_rows[:, EARLY:])
         for o in range(PASSES):
             nc.sync.dma_start(out=q_raw[o][:], in_=q_rows[o])
-        pos = keep.tile([P, Q_TILES], F32, name="pos")
-        with nc.allow_non_contiguous_dma(reason="one positive score a partition and query tile"):
-            nc.sync.dma_start(out=pos[:], in_=ps[0].rearrange("(m p) one -> p (m one)", p=P))
 
         ident = keep.tile([P, P], F32, name="ident", tag="chain1", align_bytes=64)
         make_identity(nc, ident[:])
@@ -69,48 +66,58 @@ def tile_attend_bpr_topk_kernel(tc, qT, k_words, k_scales, ib, ps, offs, out):
             nc.scalar.copy(out=bias_runs[:, b], in_=spread[:].rearrange("p i j -> p j i"))
 
         k_scale = [keep.tile([P, N], U8, name="k_scale%d" % o, align_bytes=64) for o in range(PASSES)]
-        k_code = [keep.tile([P, 2 * N], U8, name="k_code%d" % o, align_bytes=64) for o in range(PASSES)]
+        k_code = keep.tile([P, PASSES, 2 * N], U8, name="k_code", align_bytes=64)
         nc.vector.memset(k_scale[1][:].bitcast(I32), 0)
         nc.vector.tensor_copy(k_scale[0][:], scale_pool[:].indirect(offsets[:]))
         nc.sync.dma_start(out=k_scale[1][0 : P - 16, :].bitcast(I32), in_=k_scale[0][16:P, :].bitcast(I32))
+        pos = keep.tile([P, Q_TILES], F32, name="pos", tag="scales", align_bytes=64)
+        with nc.allow_non_contiguous_dma(reason="one positive score a partition and query tile"):
+            nc.sync.dma_start(out=pos[:], in_=ps[0].rearrange("(m p) one -> p (m one)", p=P))
 
-        grouped = [
-            keep.tile([P, NQ, PACK], BF16, name="grouped%d" % o, tag="chain%d" % o, align_bytes=64)
-            for o in range(PASSES)
-        ]
+        early = keep.tile([P, 3, P, PACK], BF16, name="early", tag="chain0", align_bytes=64)
+        late = keep.tile([P, P, PACK], BF16, name="late", tag="chain1", align_bytes=64)
+        grouped = {(0, 0): early[:, 0], (0, 1): early[:, 1], (1, 0): early[:, 2], (1, 1): late[:]}
         q_scale = [keep.tile([P, NQ], U8, name="q_scale%d" % o, align_bytes=64) for o in range(PASSES)]
 
-        def interleave(o, m):
-            rows = slice(m * P, (m + 1) * P)
-            nc.scalar.copy(
-                out=grouped[o][:, rows, :].rearrange("p (c i) j -> p c j i", i=4),
-                in_=q_raw[o][:, :, rows].rearrange("p j (c i) -> p c j i", i=4),
-            )
+        for o in range(PASSES):
+            for m in range(Q_TILES):
+                nc.scalar.copy(
+                    out=grouped[o, m].rearrange("p (c i) j -> p c j i", i=4),
+                    in_=q_raw[o][:, :, m * P : (m + 1) * P].rearrange("p j (c i) -> p c j i", i=4),
+                )
 
-        def quantise(o, rows):
+        word_pairs = keep.tile([P, N], U32, name="word_pairs", tag="words", align_bytes=64)
+        for h in range(2):
+            nc.vector.tensor_copy(
+                word_pairs[:, h * CHUNK : (h + 1) * CHUNK],
+                word_pool[:].indirect(offsets[:, h * 16 : (h + 1) * 16]),
+            )
+        for h in range(2):
+            nc.vector.tensor_copy(
+                k_code[:].bitcast(U16)[:, :, h * CHUNK : (h + 1) * CHUNK],
+                word_pairs[:, h * CHUNK : (h + 1) * CHUNK].bitcast(U16).rearrange("p (n o) -> p o n", o=PASSES),
+            )
+        q_code = keep.tile([P, PASSES, NQ], U32, name="q_code", tag="words", align_bytes=64)
+
+        def quantise(o, m):
+            rows = slice(m * P, (m + 1) * P)
             nc.vector.quantize_mx(
                 out=q_code[:, o, rows].bitcast(FP8X4),
                 scales=q_scale[o][:, rows],
-                in_=grouped[o][:, rows, :].rearrange("p n j -> p (n j)"),
+                in_=grouped[o, m].rearrange("p n j -> p (n j)"),
             )
 
-        for o in range(PASSES):
-            for m in range(Q_TILES):
-                interleave(o, m)
+        def gather_bias(h):
+            half = keep.tile([P, CHUNK], F32, name="bias%d" % h, tag="chain%d" % h, align_bytes=64)
+            nc.vector.tensor_copy(half[:], bias_pool[:].indirect(offsets[:, h * 16 : (h + 1) * 16]))
+            return half
 
-        word_pairs = keep.tile([P, N], U32, name="word_pairs", tag="words", align_bytes=64)
-        halves = word_pairs[:].bitcast(U16).rearrange("p (n o) -> p o n", o=PASSES)
-        nc.vector.tensor_copy(word_pairs[:], word_pool[:].indirect(offsets[:]))
-        for o in range(PASSES):
-            nc.vector.tensor_copy(k_code[o][:].bitcast(U16), halves[:, o, :])
-        q_code = keep.tile([P, PASSES, NQ], U32, name="q_code", tag="words", align_bytes=64)
-        bias = []
-        for o in range(PASSES):
-            for m in range(Q_TILES):
-                quantise(o, slice(m * P, (m + 1) * P))
-            half = keep.tile([P, CHUNK], F32, name="bias%d" % o, tag="chain%d" % o, align_bytes=64)
-            nc.vector.tensor_copy(half[:], bias_pool[:].indirect(offsets[:, o * 16 : (o + 1) * 16]))
-            bias.append(half)
+        quantise(0, 0)
+        quantise(0, 1)
+        quantise(1, 0)
+        bias = [gather_bias(0)]
+        quantise(1, 1)
+        bias.append(gather_bias(1))
 
         acc = [psum.tile([P, N], F32, name="acc%d" % m) for m in range(Q_TILES)]
         for o in range(PASSES):
@@ -119,7 +126,7 @@ def tile_attend_bpr_topk_kernel(tc, qT, k_words, k_scales, ib, ps, offs, out):
                     out=acc[m][:],
                     lhsT=q_code[:, o, m * P : (m + 1) * P].bitcast(FP8X4),
                     lhsT_scale=q_scale[o][:, m * P : (m + 1) * P],
-                    rhs=k_code[o][:].bitcast(FP4X4),
+                    rhs=k_code[:, o, :].bitcast(FP4X4),
                     rhs_scale=k_scale[o][:],
                     start=(o == 0),
                     stop=(o == PASSES - 1),

@@ -21,9 +21,11 @@ P = 128
 PACK = 4
 PASSES = D // (P * PACK)
 Q_TILES = NQ // P
-CHUNK = 256
+N_TILES = N // P
+HALF = N // 2
 EARLY = 512
 EXP_CAP = 2.0 ** 60
+STORES = [(0, 0, 128), (0, 128, 512), (1, 0, 384), (1, 384, 512)]
 
 
 def tile_attend_bpr_topk_kernel(tc, qT, k_words, k_scales, ib, ps, offs, out):
@@ -34,18 +36,20 @@ def tile_attend_bpr_topk_kernel(tc, qT, k_words, k_scales, ib, ps, offs, out):
 
         offsets = keep.tile([P, N // 16], U16, name="offsets")
         nc.sync.dma_start(offsets[:], offs)
-        bias_in = keep.tile([P, T // P], F32, name="bias_in", tag="chain0", align_bytes=64)
-        nc.sync.dma_start(out=bias_in[:], in_=ib[0].rearrange("(p c) -> p c", p=P))
+        bias_pool = keep.tile([P, T], F32, name="bias_pool", align_bytes=64)
+        nc.scalar.dma_start(out=bias_pool[P - 1 : P, :], in_=ib[0:1, :])
 
         word_pool = keep.tile([P, T], U32, name="word_pool", align_bytes=64)
         word_rows = k_words[0].rearrange("p t b -> p (t b)").bitcast(I32)
         nc.sync.dma_start(out=word_pool[:, :EARLY].bitcast(I32), in_=word_rows[:, :EARLY])
 
         scale_pool = keep.tile([P, T], U8, name="scale_pool", tag="scales", align_bytes=64)
-        nc.vector.memset(scale_pool[:].bitcast(I32), 0)
+        nc.gpsimd.memset(scale_pool[:].bitcast(I32), 0)
         scale_rows = k_scales.bitcast(I32).rearrange("o (quad r) t -> r quad o t", r=4)
         for r in range(4):
             nc.sync.dma_start(out=scale_pool[r:P:16, :].bitcast(I32), in_=scale_rows[r])
+        nc.vector.memset(bias_pool[0 : P - 1, :1408], 0.0)
+        nc.gpsimd.memset(bias_pool[0 : P - 1, 1408:], 0.0)
 
         q_raw = [keep.tile([P, PACK, NQ], F32, name="q_raw%d" % o, align_bytes=64) for o in range(PASSES)]
         q_rows = qT[0].rearrange("(o p j) n -> o p j n", p=P, j=PACK)
@@ -53,99 +57,105 @@ def tile_attend_bpr_topk_kernel(tc, qT, k_words, k_scales, ib, ps, offs, out):
         for o in range(PASSES):
             nc.sync.dma_start(out=q_raw[o][:], in_=q_rows[o])
 
-        ident = keep.tile([P, P], F32, name="ident", tag="chain1", align_bytes=64)
+        ident = keep.tile([P, P], F32, name="ident", align_bytes=64)
         make_identity(nc, ident[:])
+        scale1 = keep.tile([P, N], U8, name="scale1", align_bytes=64)
+        nc.gpsimd.memset(scale1[:].bitcast(I32), 0)
 
-        bias_pool = keep.tile([P, T], F32, name="bias_pool", align_bytes=64)
-        bias_runs = bias_pool[:].rearrange("p (j b i) -> p b j i", b=4, i=4)
-        for b in range(4):
-            spread = psum.tile([P, 4, P], F32, name="spread%d" % b)
-            for i in range(4):
-                c = 4 * b + i
-                nc.tensor.transpose(spread[:, i, :], bias_in[:, c : c + 1].to_broadcast([P, P]), ident[:])
-            nc.scalar.copy(out=bias_runs[:, b], in_=spread[:].rearrange("p i j -> p j i"))
-
-        k_scale = [keep.tile([P, N], U8, name="k_scale%d" % o, align_bytes=64) for o in range(PASSES)]
-        k_code = keep.tile([P, PASSES, 2 * N], U8, name="k_code", align_bytes=64)
-        nc.vector.memset(k_scale[1][:].bitcast(I32), 0)
-        nc.vector.tensor_copy(k_scale[0][:], scale_pool[:].indirect(offsets[:]))
-        nc.sync.dma_start(out=k_scale[1][0 : P - 16, :].bitcast(I32), in_=k_scale[0][16:P, :].bitcast(I32))
-        pos = keep.tile([P, Q_TILES], F32, name="pos", tag="scales", align_bytes=64)
+        bias = keep.tile([P, N], F32, name="bias", align_bytes=64)
+        picked = [keep.tile([P, HALF], F32, name="picked%d" % h, align_bytes=64) for h in range(2)]
+        turned = [psum.tile([P, 2, P], F32, name="turned%d" % h, tag="bank%d" % (4 + h)) for h in range(2)]
+        spread = [psum.tile([P, 2, P], F32, name="spread%d" % h, tag="bank%d" % (6 + h)) for h in range(2)]
+        columns = [keep.tile([P, 2], F32, name="columns%d" % h, tag="grouped%d" % h, align_bytes=64) for h in range(2)]
+        for h in range(2):
+            nc.vector.tensor_copy(picked[h][:], bias_pool[:].indirect(offsets[:, h * 16 : (h + 1) * 16]))
+            for c in range(2):
+                nc.tensor.transpose(turned[h][:, c, :], picked[h][:, c * P : (c + 1) * P], ident[:])
+            nc.scalar.copy(out=columns[h][:], in_=turned[h][:, :, P - 1])
+        for h in range(2):
+            for c in range(2):
+                nc.tensor.transpose(spread[h][:, c, :], columns[h][:, c : c + 1].to_broadcast([P, P]), ident[:])
+            nc.scalar.copy(out=bias[:, h * HALF : (h + 1) * HALF], in_=spread[h][:].rearrange("p c n -> p (c n)"))
+        pos = keep.tile([P, Q_TILES], F32, name="pos", tag="picked1", align_bytes=64)
         with nc.allow_non_contiguous_dma(reason="one positive score a partition and query tile"):
             nc.sync.dma_start(out=pos[:], in_=ps[0].rearrange("(m p) one -> p (m one)", p=P))
 
-        early = keep.tile([P, 3, P, PACK], BF16, name="early", tag="chain0", align_bytes=64)
-        late = keep.tile([P, P, PACK], BF16, name="late", tag="chain1", align_bytes=64)
-        grouped = {(0, 0): early[:, 0], (0, 1): early[:, 1], (1, 0): early[:, 2], (1, 1): late[:]}
-        q_scale = [keep.tile([P, NQ], U8, name="q_scale%d" % o, align_bytes=64) for o in range(PASSES)]
+        scale0 = keep.tile([P, N], U8, name="scale0", align_bytes=64)
+        nc.vector.tensor_copy(scale0[:], scale_pool[:].indirect(offsets[:]))
+        nc.sync.dma_start(out=scale1[0 : P - 16, :].bitcast(I32), in_=scale0[16:P, :].bitcast(I32))
+        k_scale = [scale0, scale1]
 
-        for o in range(PASSES):
-            for m in range(Q_TILES):
-                nc.scalar.copy(
-                    out=grouped[o, m].rearrange("p (c i) j -> p c j i", i=4),
-                    in_=q_raw[o][:, :, m * P : (m + 1) * P].rearrange("p j (c i) -> p c j i", i=4),
-                )
-
-        word_pairs = keep.tile([P, N], U32, name="word_pairs", tag="words", align_bytes=64)
+        k_code = keep.tile([P, PASSES, 2 * N], U8, name="k_code", align_bytes=64)
+        word_pairs = keep.tile([P, N], U32, name="word_pairs", align_bytes=64)
         for h in range(2):
             nc.vector.tensor_copy(
-                word_pairs[:, h * CHUNK : (h + 1) * CHUNK],
+                word_pairs[:, h * HALF : (h + 1) * HALF],
                 word_pool[:].indirect(offsets[:, h * 16 : (h + 1) * 16]),
             )
         for h in range(2):
             nc.vector.tensor_copy(
-                k_code[:].bitcast(U16)[:, :, h * CHUNK : (h + 1) * CHUNK],
-                word_pairs[:, h * CHUNK : (h + 1) * CHUNK].bitcast(U16).rearrange("p (n o) -> p o n", o=PASSES),
+                k_code[:].bitcast(U16)[:, :, h * HALF : (h + 1) * HALF],
+                word_pairs[:, h * HALF : (h + 1) * HALF].bitcast(U16).rearrange("p (n o) -> p o n", o=PASSES),
             )
-        q_code = keep.tile([P, PASSES, NQ], U32, name="q_code", tag="words", align_bytes=64)
+        q_code = keep.tile([P, PASSES, NQ], U32, name="q_code", align_bytes=64)
+        q_scale = [keep.tile([P, NQ], U8, name="q_scale%d" % o, align_bytes=64) for o in range(PASSES)]
 
-        def quantise(o, m):
+        def interleave(copy, grouped, o, lo, hi):
+            copy(
+                out=grouped[:, lo:hi, :].rearrange("p (c i) j -> p c j i", i=4),
+                in_=q_raw[o][:, :, lo:hi].rearrange("p j (c i) -> p c j i", i=4),
+            )
+
+        def quantise(grouped, o, m):
             rows = slice(m * P, (m + 1) * P)
             nc.vector.quantize_mx(
                 out=q_code[:, o, rows].bitcast(FP8X4),
                 scales=q_scale[o][:, rows],
-                in_=grouped[o, m].rearrange("p n j -> p (n j)"),
+                in_=grouped[:, rows, :].rearrange("p n j -> p (n j)"),
             )
 
-        def gather_bias(h):
-            half = keep.tile([P, CHUNK], F32, name="bias%d" % h, tag="chain%d" % h, align_bytes=64)
-            nc.vector.tensor_copy(half[:], bias_pool[:].indirect(offsets[:, h * 16 : (h + 1) * 16]))
-            return half
+        acc = [psum.tile([P, P], F32, name="acc%d" % u, tag="bank%d" % u) for u in range(Q_TILES * N_TILES)]
 
-        quantise(0, 0)
-        quantise(0, 1)
-        quantise(1, 0)
-        bias = [gather_bias(0)]
-        quantise(1, 1)
-        bias.append(gather_bias(1))
-
-        acc = [psum.tile([P, N], F32, name="acc%d" % m) for m in range(Q_TILES)]
-        for o in range(PASSES):
-            for m in range(Q_TILES):
+        def multiply(o, m):
+            for c in range(N_TILES):
                 nc.tensor.matmul_mx(
-                    out=acc[m][:],
+                    out=acc[m * N_TILES + c][:],
                     lhsT=q_code[:, o, m * P : (m + 1) * P].bitcast(FP8X4),
                     lhsT_scale=q_scale[o][:, m * P : (m + 1) * P],
-                    rhs=k_code[:, o, :].bitcast(FP4X4),
-                    rhs_scale=k_scale[o][:],
+                    rhs=k_code[:, o, 2 * c * P : 2 * (c + 1) * P].bitcast(FP4X4),
+                    rhs_scale=k_scale[o][:, c * P : (c + 1) * P],
                     start=(o == 0),
                     stop=(o == PASSES - 1),
                 )
 
-        chunks = [(m, slice(c, c + CHUNK)) for m in range(Q_TILES) for c in range(0, N, CHUNK)]
-        logit = [keep.tile([P, CHUNK], F32, name="logit%d" % u) for u in range(len(chunks))]
-        grown = keep.tile([P, len(chunks), CHUNK], F32, name="grown")
-        capped = keep.tile([P, len(chunks), CHUNK], F32, name="capped")
-        logged = [keep.tile([P, CHUNK], F32, name="logged%d" % u) for u in range(len(chunks))]
-        result = [keep.tile([P, CHUNK], F32, name="result%d" % u) for u in range(len(chunks))]
-        for u, (m, cols) in enumerate(chunks):
-            nc.vector.scalar_tensor_tensor(
-                out=logit[u][:], in0=acc[m][:, cols], scalar=pos[:, m : m + 1], in1=bias[u % 2][:],
-                op0=ALU.subtract, op1=ALU.add,
-            )
-            nc.scalar.activation(out=grown[:, u, :], in_=logit[u][:], func=ACT.Exp)
+        first = keep.tile([P, NQ, PACK], BF16, name="first", tag="grouped1", align_bytes=64)
+        interleave(nc.scalar.copy, first, 0, 0, 128)
+        interleave(nc.scalar.copy, first, 0, 128, 256)
+        for m in range(Q_TILES):
+            quantise(first, 0, m)
+            multiply(0, m)
+        second = keep.tile([P, NQ, PACK], BF16, name="second", tag="ident", align_bytes=64)
+        interleave(nc.scalar.copy, second, 1, 0, 128)
+        interleave(nc.scalar.copy, second, 1, 128, 256)
+        for m in range(Q_TILES):
+            quantise(second, 1, m)
+            multiply(1, m)
+
+        logit = keep.tile([P, Q_TILES, N], F32, name="logit")
+        grown = keep.tile([P, Q_TILES, N], F32, name="grown")
+        capped = keep.tile([P, Q_TILES, N], F32, name="capped")
+        logged = keep.tile([P, Q_TILES, N], F32, name="logged")
+        result = keep.tile([P, Q_TILES, N], F32, name="result")
+        for m in range(Q_TILES):
+            for c in range(N_TILES):
+                cols = slice(c * P, (c + 1) * P)
+                nc.vector.scalar_tensor_tensor(
+                    out=logit[:, m, cols], in0=acc[m * N_TILES + c][:], scalar=pos[:, m : m + 1], in1=bias[:, cols],
+                    op0=ALU.subtract, op1=ALU.add,
+                )
+                nc.scalar.activation(out=grown[:, m, cols], in_=logit[:, m, cols], func=ACT.Exp)
         nc.vector.tensor_scalar_min(out=capped[:], in0=grown[:], scalar1=EXP_CAP)
-        for u, (m, cols) in enumerate(chunks):
-            nc.scalar.activation(out=logged[u][:], in_=capped[:, u, :], func=ACT.Ln, bias=1.0)
-            nc.vector.tensor_tensor(out=result[u][:], in0=logged[u][:], in1=logit[u][:], op=ALU.max)
-            nc.sync.dma_start(out=out[0, m * P : (m + 1) * P, cols], in_=result[u][:])
+        for m, lo, hi in STORES:
+            nc.scalar.activation(out=logged[:, m, lo:hi], in_=capped[:, m, lo:hi], func=ACT.Ln, bias=1.0)
+            nc.vector.tensor_tensor(out=result[:, m, lo:hi], in0=logged[:, m, lo:hi], in1=logit[:, m, lo:hi], op=ALU.max)
+            nc.sync.dma_start(out=out[0, m * P : (m + 1) * P, lo:hi], in_=result[:, m, lo:hi])

@@ -25,7 +25,7 @@ N_TILES = N // P
 HALF = N // 2
 EARLY = 512
 EXP_CAP = 2.0 ** 60
-STORES = [(0, 0, 128), (0, 128, 512), (1, 0, 384), (1, 384, 512)]
+STORES = [(0, 0, 256), (0, 256, 512), (1, 0, 256), (1, 256, 384), (1, 384, 512)]
 
 
 def tile_attend_bpr_topk_kernel(tc, qT, k_words, k_scales, ib, ps, offs, out):
@@ -100,10 +100,10 @@ def tile_attend_bpr_topk_kernel(tc, qT, k_words, k_scales, ib, ps, offs, out):
         q_code = keep.tile([P, PASSES, NQ], U32, name="q_code", align_bytes=64)
         q_scale = [keep.tile([P, NQ], U8, name="q_scale%d" % o, align_bytes=64) for o in range(PASSES)]
 
-        def interleave(copy, grouped, o, lo, hi):
+        def interleave(copy, grouped, o, m):
             copy(
-                out=grouped[:, lo:hi, :].rearrange("p (c i) j -> p c j i", i=4),
-                in_=q_raw[o][:, :, lo:hi].rearrange("p j (c i) -> p c j i", i=4),
+                out=grouped.rearrange("p (c i) j -> p c j i", i=4),
+                in_=q_raw[o][:, :, m * P : (m + 1) * P].rearrange("p j (c i) -> p c j i", i=4),
             )
 
         def quantise(grouped, o, m):
@@ -111,7 +111,7 @@ def tile_attend_bpr_topk_kernel(tc, qT, k_words, k_scales, ib, ps, offs, out):
             nc.vector.quantize_mx(
                 out=q_code[:, o, rows].bitcast(FP8X4),
                 scales=q_scale[o][:, rows],
-                in_=grouped[:, rows, :].rearrange("p n j -> p (n j)"),
+                in_=grouped.rearrange("p n j -> p (n j)"),
             )
 
         acc = [psum.tile([P, P], F32, name="acc%d" % u, tag="bank%d" % u) for u in range(Q_TILES * N_TILES)]
@@ -128,17 +128,18 @@ def tile_attend_bpr_topk_kernel(tc, qT, k_words, k_scales, ib, ps, offs, out):
                     stop=(o == PASSES - 1),
                 )
 
-        first = keep.tile([P, NQ, PACK], BF16, name="first", tag="grouped1", align_bytes=64)
-        interleave(nc.scalar.copy, first, 0, 0, 128)
-        interleave(nc.scalar.copy, first, 0, 128, 256)
+        first = keep.tile([P, Q_TILES, P, PACK], BF16, name="first", tag="grouped1", align_bytes=64)
         for m in range(Q_TILES):
-            quantise(first, 0, m)
+            interleave(nc.scalar.copy, first[:, m], 0, m)
+        for m in range(Q_TILES):
+            quantise(first[:, m], 0, m)
             multiply(0, m)
-        second = keep.tile([P, NQ, PACK], BF16, name="second", tag="ident", align_bytes=64)
-        interleave(nc.scalar.copy, second, 1, 0, 128)
-        interleave(nc.scalar.copy, second, 1, 128, 256)
-        for m in range(Q_TILES):
-            quantise(second, 1, m)
+        third = keep.tile([P, P, PACK], BF16, name="third", tag="ident", align_bytes=64)
+        fourth = keep.tile([P, P, PACK], BF16, name="fourth", tag="grouped1", align_bytes=64)
+        interleave(nc.scalar.copy, third[:], 1, 0)
+        interleave(nc.vector.tensor_copy, fourth[:], 1, 1)
+        for m, grouped in enumerate((third, fourth)):
+            quantise(grouped[:], 1, m)
             multiply(1, m)
 
         logit = keep.tile([P, Q_TILES, N], F32, name="logit")
@@ -156,6 +157,8 @@ def tile_attend_bpr_topk_kernel(tc, qT, k_words, k_scales, ib, ps, offs, out):
                 nc.scalar.activation(out=grown[:, m, cols], in_=logit[:, m, cols], func=ACT.Exp)
         nc.vector.tensor_scalar_min(out=capped[:], in0=grown[:], scalar1=EXP_CAP)
         for m, lo, hi in STORES:
-            nc.scalar.activation(out=logged[:, m, lo:hi], in_=capped[:, m, lo:hi], func=ACT.Ln, bias=1.0)
-            nc.vector.tensor_tensor(out=result[:, m, lo:hi], in0=logged[:, m, lo:hi], in1=logit[:, m, lo:hi], op=ALU.max)
+            for c in range(lo, hi, P):
+                cols = slice(c, c + P)
+                nc.scalar.activation(out=logged[:, m, cols], in_=capped[:, m, cols], func=ACT.Ln, bias=1.0)
+                nc.vector.tensor_tensor(out=result[:, m, cols], in0=logged[:, m, cols], in1=logit[:, m, cols], op=ALU.max)
             nc.sync.dma_start(out=out[0, m * P : (m + 1) * P, lo:hi], in_=result[:, m, lo:hi])

@@ -76,13 +76,14 @@ def tile_attend_bpr_topk_kernel(tc, qT, k_words, k_scales, ib, ps, offs, out):
             for c in range(2):
                 nc.tensor.transpose(spread[h][:, c, :], columns[h][:, c : c + 1].to_broadcast([P, P]), ident[:])
             nc.scalar.copy(out=bias[:, h * HALF : (h + 1) * HALF], in_=spread[h][:].rearrange("p c n -> p (c n)"))
-        pos = keep.tile([P, Q_TILES], F32, name="pos", tag="picked1", align_bytes=64)
-        with nc.allow_non_contiguous_dma(reason="one positive score a partition and query tile"):
-            nc.sync.dma_start(out=pos[:], in_=ps[0].rearrange("(m p) one -> p (m one)", p=P))
 
         scale0 = keep.tile([P, N], U8, name="scale0", align_bytes=64)
         nc.vector.tensor_copy(scale0[:], scale_pool[:].indirect(offsets[:]))
-        nc.sync.dma_start(out=scale1[0 : P - 16, :].bitcast(I32), in_=scale0[16:P, :].bitcast(I32))
+        for lo, hi in ((0, 64), (64, 96), (96, 112)):
+            nc.sync.dma_start(out=scale1[lo:hi, :].bitcast(I32), in_=scale0[lo + 16 : hi + 16, :].bitcast(I32))
+        pos = keep.tile([P, Q_TILES], F32, name="pos", tag="scales", align_bytes=64)
+        with nc.allow_non_contiguous_dma(reason="one positive score a partition and query tile"):
+            nc.sync.dma_start(out=pos[:], in_=ps[0].rearrange("(m p) one -> p (m one)", p=P))
         k_scale = [scale0, scale1]
 
         k_code = keep.tile([P, PASSES, 2 * N], U8, name="k_code", align_bytes=64)

@@ -44,12 +44,11 @@ def tile_attend_bpr_topk_kernel(tc, qT, k_words, k_scales, ib, ps, offs, out):
         nc.sync.dma_start(out=word_pool[:, :EARLY].bitcast(I32), in_=word_rows[:, :EARLY])
 
         scale_pool = keep.tile([P, T], U8, name="scale_pool", tag="scales", align_bytes=64)
-        nc.gpsimd.memset(scale_pool[:].bitcast(I32), 0)
+        nc.vector.memset(scale_pool[:].bitcast(I32), 0)
         scale_rows = k_scales.bitcast(I32).rearrange("o (quad r) t -> r quad o t", r=4)
         for r in range(4):
             nc.sync.dma_start(out=scale_pool[r:P:16, :].bitcast(I32), in_=scale_rows[r])
-        nc.vector.memset(bias_pool[0 : P - 1, :1408], 0.0)
-        nc.gpsimd.memset(bias_pool[0 : P - 1, 1408:], 0.0)
+        nc.vector.memset(bias_pool[0 : P - 1, :], 0.0)
 
         q_raw = [keep.tile([P, PACK, NQ], F32, name="q_raw%d" % o, align_bytes=64) for o in range(PASSES)]
         q_rows = qT[0].rearrange("(o p j) n -> o p j n", p=P, j=PACK)

@@ -25,7 +25,7 @@ N_TILES = N // P
 HALF = N // 2
 EARLY = 512
 EXP_CAP = 2.0 ** 60
-STORES = [(0, 0, 256), (0, 256, 512), (1, 0, 256), (1, 256, 384), (1, 384, 512)]
+STORES = [(0, 0, 256), (0, 256, 512), (1, 0, 256), (1, 256, 512)]
 
 
 def tile_attend_bpr_topk_kernel(tc, qT, k_words, k_scales, ib, ps, offs, out):
@@ -100,10 +100,10 @@ def tile_attend_bpr_topk_kernel(tc, qT, k_words, k_scales, ib, ps, offs, out):
         q_code = keep.tile([P, PASSES, NQ], U32, name="q_code", align_bytes=64)
         q_scale = [keep.tile([P, NQ], U8, name="q_scale%d" % o, align_bytes=64) for o in range(PASSES)]
 
-        def interleave(copy, grouped, o, m):
+        def interleave(copy, grouped, o, lo, hi):
             copy(
                 out=grouped.rearrange("p (c i) j -> p c j i", i=4),
-                in_=q_raw[o][:, :, m * P : (m + 1) * P].rearrange("p j (c i) -> p c j i", i=4),
+                in_=q_raw[o][:, :, lo:hi].rearrange("p j (c i) -> p c j i", i=4),
             )
 
         def quantise(grouped, o, m):
@@ -128,18 +128,19 @@ def tile_attend_bpr_topk_kernel(tc, qT, k_words, k_scales, ib, ps, offs, out):
                     stop=(o == PASSES - 1),
                 )
 
-        first = keep.tile([P, Q_TILES, P, PACK], BF16, name="first", tag="grouped1", align_bytes=64)
+        grouped = keep.tile([P, 4 * P - 64, PACK], BF16, name="grouped", tag="grouped1", align_bytes=64)
+        first = [grouped[:, 0:P], grouped[:, 3 * P - 64 :]]
+        second = grouped[:, P : 3 * P]
         for m in range(Q_TILES):
-            interleave(nc.scalar.copy, first[:, m], 0, m)
+            interleave(nc.scalar.copy, first[m], 0, m * P, (m + 1) * P)
         for m in range(Q_TILES):
-            quantise(first[:, m], 0, m)
+            quantise(first[m], 0, m)
             multiply(0, m)
-        third = keep.tile([P, P, PACK], BF16, name="third", tag="ident", align_bytes=64)
-        fourth = keep.tile([P, P, PACK], BF16, name="fourth", tag="grouped1", align_bytes=64)
-        interleave(nc.scalar.copy, third[:], 1, 0)
-        interleave(nc.vector.tensor_copy, fourth[:], 1, 1)
-        for m, grouped in enumerate((third, fourth)):
-            quantise(grouped[:], 1, m)
+        interleave(nc.scalar.copy, second[:, 0:128], 1, 0, 128)
+        interleave(nc.vector.tensor_copy, second[:, 192:256], 1, 192, 256)
+        interleave(nc.scalar.copy, second[:, 128:192], 1, 128, 192)
+        for m in range(Q_TILES):
+            quantise(second[:, m * P : (m + 1) * P], 1, m)
             multiply(1, m)
 
         logit = keep.tile([P, Q_TILES, N], F32, name="logit")

@@ -37,11 +37,11 @@ def tile_attend_bpr_topk_kernel(tc, qT, k_words, k_scales, ib, ps, offs, out):
         offsets = keep.tile([P, N // 16], U16, name="offsets")
         nc.sync.dma_start(offsets[:], offs)
         bias_pool = keep.tile([P, T], F32, name="bias_pool", align_bytes=64)
-        nc.scalar.dma_start(out=bias_pool[P - 1 : P, :], in_=ib[0:1, :])
+        nc.sync.dma_start(out=bias_pool[P - 1 : P, :], in_=ib[0:1, :])
 
         word_pool = keep.tile([P, T], U32, name="word_pool", align_bytes=64)
         word_rows = k_words[0].rearrange("p t b -> p (t b)").bitcast(I32)
-        nc.sync.dma_start(out=word_pool[:, :EARLY].bitcast(I32), in_=word_rows[:, :EARLY])
+        nc.scalar.dma_start(out=word_pool[:, :EARLY].bitcast(I32), in_=word_rows[:, :EARLY])
 
         scale_pool = keep.tile([P, T], U8, name="scale_pool", tag="scales", align_bytes=64)
         nc.vector.memset(scale_pool[:].bitcast(I32), 0)
@@ -57,9 +57,10 @@ def tile_attend_bpr_topk_kernel(tc, qT, k_words, k_scales, ib, ps, offs, out):
             nc.sync.dma_start(out=q_raw[o][:], in_=q_rows[o])
 
         ident = keep.tile([P, P], F32, name="ident", align_bytes=64)
-        make_identity(nc, ident[:])
+        nc.vector.memset(ident[:], 0.0)
+        make_identity(nc, ident[:], nomemset=True)
         scale1 = keep.tile([P, N], U8, name="scale1", align_bytes=64)
-        nc.gpsimd.memset(scale1[:].bitcast(I32), 0)
+        nc.vector.memset(scale1[:].bitcast(I32), 0)
 
         bias = keep.tile([P, N], F32, name="bias", align_bytes=64)
         picked = [keep.tile([P, HALF], F32, name="picked%d" % h, align_bytes=64) for h in range(2)]

@@ -101,10 +101,10 @@ def tile_attend_bpr_topk_kernel(tc, qT, k_words, k_scales, ib, ps, offs, out):
         q_code = keep.tile([P, PASSES, NQ], U32, name="q_code", align_bytes=64)
         q_scale = [keep.tile([P, NQ], U8, name="q_scale%d" % o, align_bytes=64) for o in range(PASSES)]
 
-        def interleave(copy, grouped, o, lo, hi):
+        def interleave(copy, grouped, o, lo, hi, run=2):
             copy(
-                out=grouped.rearrange("p (c i) j -> p c j i", i=4),
-                in_=q_raw[o][:, :, lo:hi].rearrange("p j (c i) -> p c j i", i=4),
+                out=grouped.rearrange("p (c i) j -> p c j i", i=run),
+                in_=q_raw[o][:, :, lo:hi].rearrange("p j (c i) -> p c j i", i=run),
             )
 
         def quantise(grouped, o, m):
@@ -138,7 +138,7 @@ def tile_attend_bpr_topk_kernel(tc, qT, k_words, k_scales, ib, ps, offs, out):
             quantise(first[m], 0, m)
             multiply(0, m)
         interleave(nc.scalar.copy, second[:, 0:128], 1, 0, 128)
-        interleave(nc.vector.tensor_copy, second[:, 192:256], 1, 192, 256)
+        interleave(nc.vector.tensor_copy, second[:, 192:256], 1, 192, 256, 4)
         interleave(nc.scalar.copy, second[:, 128:192], 1, 128, 192)
         for m in range(Q_TILES):
             quantise(second[:, m * P : (m + 1) * P], 1, m)

@@ -129,20 +129,14 @@ def tile_attend_bpr_topk_kernel(tc, qT, k_words, k_scales, ib, ps, offs, out):
                     stop=(o == PASSES - 1),
                 )
 
-        grouped = keep.tile([P, 4 * P - 64, PACK], BF16, name="grouped", tag="grouped1", align_bytes=64)
-        first = [grouped[:, 0:P], grouped[:, 3 * P - 64 :]]
-        second = grouped[:, P : 3 * P]
-        for m in range(Q_TILES):
-            interleave(nc.scalar.copy, first[m], 0, m * P, (m + 1) * P)
-        for m in range(Q_TILES):
-            quantise(first[m], 0, m)
-            multiply(0, m)
-        interleave(nc.scalar.copy, second[:, 0:128], 1, 0, 128)
-        interleave(nc.vector.tensor_copy, second[:, 192:256], 1, 192, 256, 4)
-        interleave(nc.scalar.copy, second[:, 128:192], 1, 128, 192)
-        for m in range(Q_TILES):
-            quantise(second[:, m * P : (m + 1) * P], 1, m)
-            multiply(1, m)
+        grouped = keep.tile([P, PASSES, NQ, PACK], BF16, name="grouped", tag="grouped1", align_bytes=64)
+        for o in range(PASSES):
+            for m in range(Q_TILES):
+                interleave(nc.scalar.copy, grouped[:, o, m * P : (m + 1) * P], o, m * P, (m + 1) * P)
+        for o in range(PASSES):
+            for m in range(Q_TILES):
+                quantise(grouped[:, o, m * P : (m + 1) * P], o, m)
+                multiply(o, m)
 
         logit = keep.tile([P, Q_TILES, N], F32, name="logit")
         grown = keep.tile([P, Q_TILES, N], F32, name="grown")

@@ -22,10 +22,18 @@ PACK = 4
 PASSES = D // (P * PACK)
 Q_TILES = NQ // P
 N_TILES = N // P
-HALF = N // 2
+HALVES = 2
+HALF = N // HALVES
+HALF_TILES = HALF // P
+LIST_ROWS = 16
+HALF_COLS = HALF // LIST_ROWS
+SCALE_ROWS = 4
+PASS_SHIFT = 16
+SHIFT_RUNS = ((0, 64), (64, 96), (96, 112))
 EARLY = 512
+RUN = 2
 EXP_CAP = 2.0 ** 60
-STORES = [(0, 0, 256), (0, 256, 512), (1, 0, 256), (1, 256, 512)]
+STORES = [(0, 0, 128), (0, 128, 384), (0, 384, 512), (1, 0, 256), (1, 256, 512)]
 
 
 def tile_attend_bpr_topk_kernel(tc, qT, k_words, k_scales, ib, ps, offs, out):
@@ -34,7 +42,10 @@ def tile_attend_bpr_topk_kernel(tc, qT, k_words, k_scales, ib, ps, offs, out):
         keep = ctx.enter_context(tc.tile_pool(name="keep", bufs=1))
         psum = ctx.enter_context(tc.psum_pool(name="psum", bufs=1))
 
-        offsets = keep.tile([P, N // 16], U16, name="offsets")
+        def list_half(h):
+            return offsets[:, h * HALF_COLS : (h + 1) * HALF_COLS]
+
+        offsets = keep.tile([P, N // LIST_ROWS], U16, name="offsets")
         nc.sync.dma_start(offsets[:], offs)
         bias_pool = keep.tile([P, T], F32, name="bias_pool", align_bytes=64)
         nc.sync.dma_start(out=bias_pool[P - 1 : P, :], in_=ib[0:1, :])
@@ -45,9 +56,9 @@ def tile_attend_bpr_topk_kernel(tc, qT, k_words, k_scales, ib, ps, offs, out):
 
         scale_pool = keep.tile([P, T], U8, name="scale_pool", tag="scales", align_bytes=64)
         nc.vector.memset(scale_pool[:].bitcast(I32), 0)
-        scale_rows = k_scales.bitcast(I32).rearrange("o (quad r) t -> r quad o t", r=4)
-        for r in range(4):
-            nc.sync.dma_start(out=scale_pool[r:P:16, :].bitcast(I32), in_=scale_rows[r])
+        scale_rows = k_scales.bitcast(I32).rearrange("o (quad r) t -> r quad o t", r=SCALE_ROWS)
+        for r in range(SCALE_ROWS):
+            nc.sync.dma_start(out=scale_pool[r:P:PASS_SHIFT, :].bitcast(I32), in_=scale_rows[r])
         nc.vector.memset(bias_pool[0 : P - 1, :], 0.0)
 
         q_raw = [keep.tile([P, PACK, NQ], F32, name="q_raw%d" % o, align_bytes=64) for o in range(PASSES)]
@@ -63,24 +74,35 @@ def tile_attend_bpr_topk_kernel(tc, qT, k_words, k_scales, ib, ps, offs, out):
         nc.vector.memset(scale1[:].bitcast(I32), 0)
 
         bias = keep.tile([P, N], F32, name="bias", align_bytes=64)
-        picked = [keep.tile([P, HALF], F32, name="picked%d" % h, align_bytes=64) for h in range(2)]
-        turned = [psum.tile([P, 2, P], F32, name="turned%d" % h, tag="bank%d" % (4 + h)) for h in range(2)]
-        spread = [psum.tile([P, 2, P], F32, name="spread%d" % h, tag="bank%d" % (6 + h)) for h in range(2)]
-        columns = [keep.tile([P, 2], F32, name="columns%d" % h, tag="grouped%d" % h, align_bytes=64) for h in range(2)]
-        for h in range(2):
-            nc.vector.tensor_copy(picked[h][:], bias_pool[:].indirect(offsets[:, h * 16 : (h + 1) * 16]))
-            for c in range(2):
+        picked = [keep.tile([P, HALF], F32, name="picked%d" % h, align_bytes=64) for h in range(HALVES)]
+        turned = [
+            psum.tile([P, HALF_TILES, P], F32, name="turned%d" % h, tag="bank%d" % (N_TILES + h))
+            for h in range(HALVES)
+        ]
+        spread = [
+            psum.tile([P, HALF_TILES, P], F32, name="spread%d" % h, tag="bank%d" % (N_TILES + HALVES + h))
+            for h in range(HALVES)
+        ]
+        columns = [
+            keep.tile([P, HALF_TILES], F32, name="columns%d" % h, tag="columns%d" % h, align_bytes=64)
+            for h in range(HALVES)
+        ]
+        for h in range(HALVES):
+            nc.vector.tensor_copy(picked[h][:], bias_pool[:].indirect(list_half(h)))
+            for c in range(HALF_TILES):
                 nc.tensor.transpose(turned[h][:, c, :], picked[h][:, c * P : (c + 1) * P], ident[:])
             nc.scalar.copy(out=columns[h][:], in_=turned[h][:, :, P - 1])
-        for h in range(2):
-            for c in range(2):
+        for h in range(HALVES):
+            for c in range(HALF_TILES):
                 nc.tensor.transpose(spread[h][:, c, :], columns[h][:, c : c + 1].to_broadcast([P, P]), ident[:])
             nc.scalar.copy(out=bias[:, h * HALF : (h + 1) * HALF], in_=spread[h][:].rearrange("p c n -> p (c n)"))
 
         scale0 = keep.tile([P, N], U8, name="scale0", align_bytes=64)
         nc.vector.tensor_copy(scale0[:], scale_pool[:].indirect(offsets[:]))
-        for lo, hi in ((0, 64), (64, 96), (96, 112)):
-            nc.sync.dma_start(out=scale1[lo:hi, :].bitcast(I32), in_=scale0[lo + 16 : hi + 16, :].bitcast(I32))
+        for lo, hi in SHIFT_RUNS:
+            nc.sync.dma_start(
+                out=scale1[lo:hi, :].bitcast(I32), in_=scale0[lo + PASS_SHIFT : hi + PASS_SHIFT, :].bitcast(I32)
+            )
         pos = keep.tile([P, Q_TILES], F32, name="pos", tag="scales", align_bytes=64)
         with nc.allow_non_contiguous_dma(reason="one positive score a partition and query tile"):
             nc.sync.dma_start(out=pos[:], in_=ps[0].rearrange("(m p) one -> p (m one)", p=P))
@@ -88,55 +110,43 @@ def tile_attend_bpr_topk_kernel(tc, qT, k_words, k_scales, ib, ps, offs, out):
 
         k_code = keep.tile([P, PASSES, 2 * N], U8, name="k_code", align_bytes=64)
         word_pairs = keep.tile([P, N], U32, name="word_pairs", align_bytes=64)
-        for h in range(2):
-            nc.vector.tensor_copy(
-                word_pairs[:, h * HALF : (h + 1) * HALF],
-                word_pool[:].indirect(offsets[:, h * 16 : (h + 1) * 16]),
-            )
-        for h in range(2):
+        for h in range(HALVES):
+            nc.vector.tensor_copy(word_pairs[:, h * HALF : (h + 1) * HALF], word_pool[:].indirect(list_half(h)))
+        for h in range(HALVES):
             nc.vector.tensor_copy(
                 k_code[:].bitcast(U16)[:, :, h * HALF : (h + 1) * HALF],
                 word_pairs[:, h * HALF : (h + 1) * HALF].bitcast(U16).rearrange("p (n o) -> p o n", o=PASSES),
             )
+
         q_code = keep.tile([P, PASSES, NQ], U32, name="q_code", align_bytes=64)
         q_scale = [keep.tile([P, NQ], U8, name="q_scale%d" % o, align_bytes=64) for o in range(PASSES)]
-
-        def interleave(copy, grouped, o, lo, hi, run=2):
-            copy(
-                out=grouped.rearrange("p (c i) j -> p c j i", i=run),
-                in_=q_raw[o][:, :, lo:hi].rearrange("p j (c i) -> p c j i", i=run),
-            )
-
-        def quantise(grouped, o, m):
-            rows = slice(m * P, (m + 1) * P)
-            nc.vector.quantize_mx(
-                out=q_code[:, o, rows].bitcast(FP8X4),
-                scales=q_scale[o][:, rows],
-                in_=grouped.rearrange("p n j -> p (n j)"),
-            )
-
         acc = [psum.tile([P, P], F32, name="acc%d" % u, tag="bank%d" % u) for u in range(Q_TILES * N_TILES)]
-
-        def multiply(o, m):
-            for c in range(N_TILES):
-                nc.tensor.matmul_mx(
-                    out=acc[m * N_TILES + c][:],
-                    lhsT=q_code[:, o, m * P : (m + 1) * P].bitcast(FP8X4),
-                    lhsT_scale=q_scale[o][:, m * P : (m + 1) * P],
-                    rhs=k_code[:, o, 2 * c * P : 2 * (c + 1) * P].bitcast(FP4X4),
-                    rhs_scale=k_scale[o][:, c * P : (c + 1) * P],
-                    start=(o == 0),
-                    stop=(o == PASSES - 1),
+        grouped = keep.tile([P, PASSES, NQ, PACK], BF16, name="grouped", tag="columns1", align_bytes=64)
+        for o in range(PASSES):
+            for m in range(Q_TILES):
+                rows = slice(m * P, (m + 1) * P)
+                nc.scalar.copy(
+                    out=grouped[:, o, rows].rearrange("p (c i) j -> p c j i", i=RUN),
+                    in_=q_raw[o][:, :, rows].rearrange("p j (c i) -> p c j i", i=RUN),
                 )
-
-        grouped = keep.tile([P, PASSES, NQ, PACK], BF16, name="grouped", tag="grouped1", align_bytes=64)
         for o in range(PASSES):
             for m in range(Q_TILES):
-                interleave(nc.scalar.copy, grouped[:, o, m * P : (m + 1) * P], o, m * P, (m + 1) * P)
-        for o in range(PASSES):
-            for m in range(Q_TILES):
-                quantise(grouped[:, o, m * P : (m + 1) * P], o, m)
-                multiply(o, m)
+                rows = slice(m * P, (m + 1) * P)
+                nc.vector.quantize_mx(
+                    out=q_code[:, o, rows].bitcast(FP8X4),
+                    scales=q_scale[o][:, rows],
+                    in_=grouped[:, o, rows].rearrange("p n j -> p (n j)"),
+                )
+                for c in range(N_TILES):
+                    nc.tensor.matmul_mx(
+                        out=acc[m * N_TILES + c][:],
+                        lhsT=q_code[:, o, rows].bitcast(FP8X4),
+                        lhsT_scale=q_scale[o][:, rows],
+                        rhs=k_code[:, o, 2 * c * P : 2 * (c + 1) * P].bitcast(FP4X4),
+                        rhs_scale=k_scale[o][:, c * P : (c + 1) * P],
+                        start=(o == 0),
+                        stop=(o == PASSES - 1),
+                    )
 
         logit = keep.tile([P, Q_TILES, N], F32, name="logit")
         grown = keep.tile([P, Q_TILES, N], F32, name="grown")
@@ -153,8 +163,8 @@ def tile_attend_bpr_topk_kernel(tc, qT, k_words, k_scales, ib, ps, offs, out):
                 nc.scalar.activation(out=grown[:, m, cols], in_=logit[:, m, cols], func=ACT.Exp)
         nc.vector.tensor_scalar_min(out=capped[:], in0=grown[:], scalar1=EXP_CAP)
         for m, lo, hi in STORES:
-            for c in range(lo, hi, P):
-                cols = slice(c, c + P)
+            for first in range(lo, hi, P):
+                cols = slice(first, first + P)
                 nc.scalar.activation(out=logged[:, m, cols], in_=capped[:, m, cols], func=ACT.Ln, bias=1.0)
                 nc.vector.tensor_tensor(out=result[:, m, cols], in0=logged[:, m, cols], in1=logit[:, m, cols], op=ALU.max)
             nc.sync.dma_start(out=out[0, m * P : (m + 1) * P, lo:hi], in_=result[:, m, lo:hi])

@@ -31,6 +31,9 @@ SCALE_ROWS = 4
 PASS_SHIFT = 16
 SHIFT_RUNS = ((0, 64), (64, 96), (96, 112))
 EARLY = 512
+PIECE = 1024
+SHARE_FIRST = 96
+SHARE_LAST = 64
 RUN = 2
 EXP_CAP = 2.0 ** 60
 STORES = [(0, 0, 128), (0, 128, 384), (0, 384, 512), (1, 0, 256), (1, 256, 512)]
@@ -40,6 +43,7 @@ def tile_attend_bpr_topk_kernel(tc, qT, k_words, k_scales, ib, ps, offs, out):
     nc = tc.nc
     with ExitStack() as ctx:
         keep = ctx.enter_context(tc.tile_pool(name="keep", bufs=1))
+        reuse = ctx.enter_context(tc.tile_pool(name="reuse", bufs=1))
         psum = ctx.enter_context(tc.psum_pool(name="psum", bufs=1))
 
         def list_half(h):
@@ -48,11 +52,11 @@ def tile_attend_bpr_topk_kernel(tc, qT, k_words, k_scales, ib, ps, offs, out):
         offsets = keep.tile([P, N // LIST_ROWS], U16, name="offsets")
         nc.sync.dma_start(offsets[:], offs)
         bias_pool = keep.tile([P, T], F32, name="bias_pool", align_bytes=64)
-        nc.sync.dma_start(out=bias_pool[P - 1 : P, :], in_=ib[0:1, :])
+        nc.scalar.dma_start(out=bias_pool[P - 1 : P, :], in_=ib[0:1, :])
 
         word_pool = keep.tile([P, T], U32, name="word_pool", align_bytes=64)
         word_rows = k_words[0].rearrange("p t b -> p (t b)").bitcast(I32)
-        nc.scalar.dma_start(out=word_pool[:, :EARLY].bitcast(I32), in_=word_rows[:, :EARLY])
+        nc.sync.dma_start(out=word_pool[:, :EARLY].bitcast(I32), in_=word_rows[:, :EARLY])
 
         scale_pool = keep.tile([P, T], U8, name="scale_pool", tag="scales", align_bytes=64)
         nc.vector.memset(scale_pool[:].bitcast(I32), 0)
@@ -61,7 +65,10 @@ def tile_attend_bpr_topk_kernel(tc, qT, k_words, k_scales, ib, ps, offs, out):
             nc.sync.dma_start(out=scale_pool[r:P:PASS_SHIFT, :].bitcast(I32), in_=scale_rows[r])
         nc.vector.memset(bias_pool[0 : P - 1, :], 0.0)
 
-        q_raw = [keep.tile([P, PACK, NQ], F32, name="q_raw%d" % o, align_bytes=64) for o in range(PASSES)]
+        q_raw = [
+            reuse.tile([P, PACK, NQ], F32, name="q_raw0", align_bytes=64, offset=4 * PIECE),
+            keep.tile([P, PACK, NQ], F32, name="q_raw1", align_bytes=64),
+        ]
         q_rows = qT[0].rearrange("(o p j) n -> o p j n", p=P, j=PACK)
         nc.sync.dma_start(out=word_pool[:, EARLY:].bitcast(I32), in_=word_rows[:, EARLY:])
         for o in range(PASSES):
@@ -71,7 +78,7 @@ def tile_attend_bpr_topk_kernel(tc, qT, k_words, k_scales, ib, ps, offs, out):
         nc.vector.memset(ident[:], 0.0)
         make_identity(nc, ident[:], nomemset=True)
         scale1 = keep.tile([P, N], U8, name="scale1", align_bytes=64)
-        nc.vector.memset(scale1[:].bitcast(I32), 0)
+        nc.gpsimd.memset(scale1[:].bitcast(I32), 0)
 
         bias = keep.tile([P, N], F32, name="bias", align_bytes=64)
         picked = [keep.tile([P, HALF], F32, name="picked%d" % h, align_bytes=64) for h in range(HALVES)]
@@ -84,14 +91,14 @@ def tile_attend_bpr_topk_kernel(tc, qT, k_words, k_scales, ib, ps, offs, out):
             for h in range(HALVES)
         ]
         columns = [
-            keep.tile([P, HALF_TILES], F32, name="columns%d" % h, tag="columns%d" % h, align_bytes=64)
-            for h in range(HALVES)
+            keep.tile([P, HALF_TILES], F32, name="columns0", align_bytes=64)[:],
+            reuse.tile([P, 4 * PIECE // 4], F32, name="columns1", align_bytes=64, offset=0)[:, :HALF_TILES],
         ]
         for h in range(HALVES):
             nc.vector.tensor_copy(picked[h][:], bias_pool[:].indirect(list_half(h)))
             for c in range(HALF_TILES):
                 nc.tensor.transpose(turned[h][:, c, :], picked[h][:, c * P : (c + 1) * P], ident[:])
-            nc.scalar.copy(out=columns[h][:], in_=turned[h][:, :, P - 1])
+            nc.scalar.copy(out=columns[h], in_=turned[h][:, :, P - 1])
         for h in range(HALVES):
             for c in range(HALF_TILES):
                 nc.tensor.transpose(spread[h][:, c, :], columns[h][:, c : c + 1].to_broadcast([P, P]), ident[:])
@@ -108,41 +115,57 @@ def tile_attend_bpr_topk_kernel(tc, qT, k_words, k_scales, ib, ps, offs, out):
             nc.sync.dma_start(out=pos[:], in_=ps[0].rearrange("(m p) one -> p (m one)", p=P))
         k_scale = [scale0, scale1]
 
-        k_code = keep.tile([P, PASSES, 2 * N], U8, name="k_code", align_bytes=64)
         word_pairs = keep.tile([P, N], U32, name="word_pairs", align_bytes=64)
-        for h in range(HALVES):
-            nc.vector.tensor_copy(word_pairs[:, h * HALF : (h + 1) * HALF], word_pool[:].indirect(list_half(h)))
-        for h in range(HALVES):
-            nc.vector.tensor_copy(
-                k_code[:].bitcast(U16)[:, :, h * HALF : (h + 1) * HALF],
-                word_pairs[:, h * HALF : (h + 1) * HALF].bitcast(U16).rearrange("p (n o) -> p o n", o=PASSES),
-            )
-
+        by_pass = word_pairs[:].bitcast(U16).rearrange("p (n o) -> p o n", o=PASSES)
+        k_first = reuse.tile([P, 2 * N], U8, name="k_first", align_bytes=64, offset=3 * PIECE)
         q_code = keep.tile([P, PASSES, NQ], U32, name="q_code", align_bytes=64)
         q_scale = [keep.tile([P, NQ], U8, name="q_scale%d" % o, align_bytes=64) for o in range(PASSES)]
+        grouped = [
+            reuse.tile([P, P, PACK], BF16, name="grouped%d" % u, align_bytes=64, offset=u * PIECE)
+            for u in range(PASSES * Q_TILES - 1)
+        ]
+
+        def interleave(copy, o, m, lo, hi):
+            copy(
+                out=grouped[o * Q_TILES + m][:, lo:hi].rearrange("p (c i) j -> p c j i", i=RUN),
+                in_=q_raw[o][:, :, m * P + lo : m * P + hi].rearrange("p j (c i) -> p c j i", i=RUN),
+            )
+
+        def quantise(o, m):
+            rows = slice(m * P, (m + 1) * P)
+            nc.vector.quantize_mx(
+                out=q_code[:, o, rows].bitcast(FP8X4),
+                scales=q_scale[o][:, rows],
+                in_=grouped[o * Q_TILES + m][:].rearrange("p n j -> p (n j)"),
+            )
+
+        nc.vector.tensor_copy(word_pairs[:], word_pool[:].indirect(offsets[:]))
+        interleave(nc.vector.tensor_copy, 0, 0, 0, SHARE_FIRST)
+        interleave(nc.scalar.copy, 0, 0, SHARE_FIRST, P)
+        nc.vector.tensor_copy(k_first[:].bitcast(U16), by_pass[:, 0, :])
+        quantise(0, 0)
+        interleave(nc.scalar.copy, 0, 1, 0, P)
+        quantise(0, 1)
+        k_second = reuse.tile([P, 2 * N], U8, name="k_second", align_bytes=64, offset=4 * PIECE)
+        grouped.append(reuse.tile([P, P, PACK], BF16, name="grouped_last", align_bytes=64, offset=5 * PIECE))
+        nc.vector.tensor_copy(k_second[:].bitcast(U16), by_pass[:, 1, :])
+        interleave(nc.scalar.copy, 1, 0, 0, P)
+        interleave(nc.vector.tensor_copy, 1, 1, 0, SHARE_LAST)
+        interleave(nc.scalar.copy, 1, 1, SHARE_LAST, P)
+        quantise(1, 0)
+        quantise(1, 1)
+
+        k_code = [k_first, k_second]
         acc = [psum.tile([P, P], F32, name="acc%d" % u, tag="bank%d" % u) for u in range(Q_TILES * N_TILES)]
-        grouped = keep.tile([P, PASSES, NQ, PACK], BF16, name="grouped", tag="columns1", align_bytes=64)
         for o in range(PASSES):
             for m in range(Q_TILES):
                 rows = slice(m * P, (m + 1) * P)
-                nc.scalar.copy(
-                    out=grouped[:, o, rows].rearrange("p (c i) j -> p c j i", i=RUN),
-                    in_=q_raw[o][:, :, rows].rearrange("p j (c i) -> p c j i", i=RUN),
-                )
-        for o in range(PASSES):
-            for m in range(Q_TILES):
-                rows = slice(m * P, (m + 1) * P)
-                nc.vector.quantize_mx(
-                    out=q_code[:, o, rows].bitcast(FP8X4),
-                    scales=q_scale[o][:, rows],
-                    in_=grouped[:, o, rows].rearrange("p n j -> p (n j)"),
-                )
                 for c in range(N_TILES):
                     nc.tensor.matmul_mx(
                         out=acc[m * N_TILES + c][:],
                         lhsT=q_code[:, o, rows].bitcast(FP8X4),
                         lhsT_scale=q_scale[o][:, rows],
-                        rhs=k_code[:, o, 2 * c * P : 2 * (c + 1) * P].bitcast(FP4X4),
+                        rhs=k_code[o][:, 2 * c * P : 2 * (c + 1) * P].bitcast(FP4X4),
                         rhs_scale=k_scale[o][:, c * P : (c + 1) * P],
                         start=(o == 0),
                         stop=(o == PASSES - 1),

@@ -32,8 +32,7 @@ PASS_SHIFT = 16
 SHIFT_RUNS = ((0, 64), (64, 96), (96, 112))
 EARLY = 512
 PIECE = 1024
-SHARE_FIRST = 96
-SHARE_LAST = 64
+SHARE = 96
 RUN = 2
 EXP_CAP = 2.0 ** 60
 STORES = [(0, 0, 128), (0, 128, 384), (0, 384, 512), (1, 0, 256), (1, 256, 512)]
@@ -66,7 +65,7 @@ def tile_attend_bpr_topk_kernel(tc, qT, k_words, k_scales, ib, ps, offs, out):
         nc.vector.memset(bias_pool[0 : P - 1, :], 0.0)
 
         q_raw = [
-            reuse.tile([P, PACK, NQ], F32, name="q_raw0", align_bytes=64, offset=4 * PIECE),
+            reuse.tile([P, PACK, NQ], F32, name="q_raw0", align_bytes=64, offset=3 * PIECE),
             keep.tile([P, PACK, NQ], F32, name="q_raw1", align_bytes=64),
         ]
         q_rows = qT[0].rearrange("(o p j) n -> o p j n", p=P, j=PACK)
@@ -92,7 +91,7 @@ def tile_attend_bpr_topk_kernel(tc, qT, k_words, k_scales, ib, ps, offs, out):
         ]
         columns = [
             keep.tile([P, HALF_TILES], F32, name="columns0", align_bytes=64)[:],
-            reuse.tile([P, 4 * PIECE // 4], F32, name="columns1", align_bytes=64, offset=0)[:, :HALF_TILES],
+            reuse.tile([P, 3 * PIECE // 4], F32, name="columns1", align_bytes=64, offset=0)[:, :HALF_TILES],
         ]
         for h in range(HALVES):
             nc.vector.tensor_copy(picked[h][:], bias_pool[:].indirect(list_half(h)))
@@ -117,12 +116,12 @@ def tile_attend_bpr_topk_kernel(tc, qT, k_words, k_scales, ib, ps, offs, out):
 
         word_pairs = keep.tile([P, N], U32, name="word_pairs", align_bytes=64)
         by_pass = word_pairs[:].bitcast(U16).rearrange("p (n o) -> p o n", o=PASSES)
-        k_first = reuse.tile([P, 2 * N], U8, name="k_first", align_bytes=64, offset=3 * PIECE)
+        k_first = reuse.tile([P, 2 * N], U8, name="k_first", align_bytes=64, offset=2 * PIECE)
         q_code = keep.tile([P, PASSES, NQ], U32, name="q_code", align_bytes=64)
         q_scale = [keep.tile([P, NQ], U8, name="q_scale%d" % o, align_bytes=64) for o in range(PASSES)]
         grouped = [
             reuse.tile([P, P, PACK], BF16, name="grouped%d" % u, align_bytes=64, offset=u * PIECE)
-            for u in range(PASSES * Q_TILES - 1)
+            for u in range(Q_TILES)
         ]
 
         def interleave(copy, o, m, lo, hi):
@@ -140,18 +139,19 @@ def tile_attend_bpr_topk_kernel(tc, qT, k_words, k_scales, ib, ps, offs, out):
             )
 
         nc.vector.tensor_copy(word_pairs[:], word_pool[:].indirect(offsets[:]))
-        interleave(nc.vector.tensor_copy, 0, 0, 0, SHARE_FIRST)
-        interleave(nc.scalar.copy, 0, 0, SHARE_FIRST, P)
+        interleave(nc.vector.tensor_copy, 0, 0, 0, SHARE)
+        interleave(nc.scalar.copy, 0, 0, SHARE, P)
         nc.vector.tensor_copy(k_first[:].bitcast(U16), by_pass[:, 0, :])
         quantise(0, 0)
         interleave(nc.scalar.copy, 0, 1, 0, P)
         quantise(0, 1)
-        k_second = reuse.tile([P, 2 * N], U8, name="k_second", align_bytes=64, offset=4 * PIECE)
-        grouped.append(reuse.tile([P, P, PACK], BF16, name="grouped_last", align_bytes=64, offset=5 * PIECE))
+        k_second = reuse.tile([P, 2 * N], U8, name="k_second", align_bytes=64, offset=3 * PIECE)
+        second = reuse.tile([P, Q_TILES, P, PACK], BF16, name="grouped_second", align_bytes=64, offset=4 * PIECE)
+        grouped.extend(second[:, m] for m in range(Q_TILES))
         nc.vector.tensor_copy(k_second[:].bitcast(U16), by_pass[:, 1, :])
-        interleave(nc.scalar.copy, 1, 0, 0, P)
-        interleave(nc.vector.tensor_copy, 1, 1, 0, SHARE_LAST)
-        interleave(nc.scalar.copy, 1, 1, SHARE_LAST, P)
+        interleave(nc.vector.tensor_copy, 1, 0, 0, SHARE)
+        interleave(nc.scalar.copy, 1, 0, SHARE, P)
+        interleave(nc.scalar.copy, 1, 1, 0, P)
         quantise(1, 0)
         quantise(1, 1)
 

@@ -148,8 +148,8 @@ def tile_attend_bpr_topk_kernel(tc, qT, k_words, k_scales, ib, ps, offs, out):
         k_second = reuse.tile([P, 2 * N], U8, name="k_second", align_bytes=64, offset=3 * PIECE)
         second = reuse.tile([P, Q_TILES, P, PACK], BF16, name="grouped_second", align_bytes=64, offset=4 * PIECE)
         grouped.extend(second[:, m] for m in range(Q_TILES))
-        nc.vector.tensor_copy(k_second[:].bitcast(U16), by_pass[:, 1, :])
         interleave(nc.vector.tensor_copy, 1, 0, 0, SHARE)
+        nc.vector.tensor_copy(k_second[:].bitcast(U16), by_pass[:, 1, :])
         interleave(nc.scalar.copy, 1, 0, SHARE, P)
         interleave(nc.scalar.copy, 1, 1, 0, P)
         quantise(1, 0)

@@ -32,7 +32,7 @@ PASS_SHIFT = 16
 SHIFT_RUNS = ((0, 64), (64, 96), (96, 112))
 EARLY = 512
 PIECE = 1024
-SHARE = 96
+SHARE = (64, 96)
 RUN = 2
 EXP_CAP = 2.0 ** 60
 STORES = [(0, 0, 128), (0, 128, 384), (0, 384, 512), (1, 0, 256), (1, 256, 512)]
@@ -77,7 +77,7 @@ def tile_attend_bpr_topk_kernel(tc, qT, k_words, k_scales, ib, ps, offs, out):
         nc.vector.memset(ident[:], 0.0)
         make_identity(nc, ident[:], nomemset=True)
         scale1 = keep.tile([P, N], U8, name="scale1", align_bytes=64)
-        nc.gpsimd.memset(scale1[:].bitcast(I32), 0)
+        nc.vector.memset(scale1[:].bitcast(I32), 0)
 
         bias = keep.tile([P, N], F32, name="bias", align_bytes=64)
         picked = [keep.tile([P, HALF], F32, name="picked%d" % h, align_bytes=64) for h in range(HALVES)]
@@ -139,8 +139,8 @@ def tile_attend_bpr_topk_kernel(tc, qT, k_words, k_scales, ib, ps, offs, out):
             )
 
         nc.vector.tensor_copy(word_pairs[:], word_pool[:].indirect(offsets[:]))
-        interleave(nc.vector.tensor_copy, 0, 0, 0, SHARE)
-        interleave(nc.scalar.copy, 0, 0, SHARE, P)
+        interleave(nc.vector.tensor_copy, 0, 0, 0, SHARE[0])
+        interleave(nc.scalar.copy, 0, 0, SHARE[0], P)
         nc.vector.tensor_copy(k_first[:].bitcast(U16), by_pass[:, 0, :])
         quantise(0, 0)
         interleave(nc.scalar.copy, 0, 1, 0, P)
@@ -148,9 +148,9 @@ def tile_attend_bpr_topk_kernel(tc, qT, k_words, k_scales, ib, ps, offs, out):
         k_second = reuse.tile([P, 2 * N], U8, name="k_second", align_bytes=64, offset=3 * PIECE)
         second = reuse.tile([P, Q_TILES, P, PACK], BF16, name="grouped_second", align_bytes=64, offset=4 * PIECE)
         grouped.extend(second[:, m] for m in range(Q_TILES))
-        interleave(nc.vector.tensor_copy, 1, 0, 0, SHARE)
+        interleave(nc.vector.tensor_copy, 1, 0, 0, SHARE[1])
         nc.vector.tensor_copy(k_second[:].bitcast(U16), by_pass[:, 1, :])
-        interleave(nc.scalar.copy, 1, 0, SHARE, P)
+        interleave(nc.scalar.copy, 1, 0, SHARE[1], P)
         interleave(nc.scalar.copy, 1, 1, 0, P)
         quantise(1, 0)
         quantise(1, 1)

@@ -50,14 +50,14 @@ def tile_attend_bpr_topk_kernel(tc, qT, k_words, k_scales, ib, ps, offs, out):
 
         offsets = keep.tile([P, N // LIST_ROWS], U16, name="offsets")
         nc.sync.dma_start(offsets[:], offs)
-        bias_pool = keep.tile([P, T], F32, name="bias_pool", align_bytes=64)
+        bias_pool = keep.tile([P, T], F32, name="bias_pool", align_bytes=256)
         nc.scalar.dma_start(out=bias_pool[P - 1 : P, :], in_=ib[0:1, :])
 
-        word_pool = keep.tile([P, T], U32, name="word_pool", align_bytes=64)
+        word_pool = keep.tile([P, T], U32, name="word_pool", align_bytes=256)
         word_rows = k_words[0].rearrange("p t b -> p (t b)").bitcast(I32)
         nc.sync.dma_start(out=word_pool[:, :EARLY].bitcast(I32), in_=word_rows[:, :EARLY])
 
-        scale_pool = keep.tile([P, T], U8, name="scale_pool", tag="scales", align_bytes=64)
+        scale_pool = keep.tile([P, T], U8, name="scale_pool", tag="scales", align_bytes=256)
         nc.vector.memset(scale_pool[:].bitcast(I32), 0)
         scale_rows = k_scales.bitcast(I32).rearrange("o (quad r) t -> r quad o t", r=SCALE_ROWS)
         for r in range(SCALE_ROWS):
@@ -65,8 +65,8 @@ def tile_attend_bpr_topk_kernel(tc, qT, k_words, k_scales, ib, ps, offs, out):
         nc.vector.memset(bias_pool[0 : P - 1, :], 0.0)
 
         q_raw = [
-            reuse.tile([P, PACK, NQ], F32, name="q_raw0", align_bytes=64, offset=3 * PIECE),
-            keep.tile([P, PACK, NQ], F32, name="q_raw1", align_bytes=64),
+            reuse.tile([P, PACK, NQ], F32, name="q_raw0", align_bytes=256, offset=3 * PIECE),
+            keep.tile([P, PACK, NQ], F32, name="q_raw1", align_bytes=256),
         ]
         q_rows = qT[0].rearrange("(o p j) n -> o p j n", p=P, j=PACK)
         nc.sync.dma_start(out=word_pool[:, EARLY:].bitcast(I32), in_=word_rows[:, EARLY:])
@@ -109,7 +109,7 @@ def tile_attend_bpr_topk_kernel(tc, qT, k_words, k_scales, ib, ps, offs, out):
             nc.sync.dma_start(
                 out=scale1[lo:hi, :].bitcast(I32), in_=scale0[lo + PASS_SHIFT : hi + PASS_SHIFT, :].bitcast(I32)
             )
-        pos = keep.tile([P, Q_TILES], F32, name="pos", tag="scales", align_bytes=64)
+        pos = keep.tile([P, Q_TILES], F32, name="pos", tag="scales", align_bytes=256)
         with nc.allow_non_contiguous_dma(reason="one positive score a partition and query tile"):
             nc.sync.dma_start(out=pos[:], in_=ps[0].rearrange("(m p) one -> p (m one)", p=P))
         k_scale = [scale0, scale1]
@@ -175,7 +175,7 @@ def tile_attend_bpr_topk_kernel(tc, qT, k_words, k_scales, ib, ps, offs, out):
         grown = keep.tile([P, Q_TILES, N], F32, name="grown")
         capped = keep.tile([P, Q_TILES, N], F32, name="capped")
         logged = keep.tile([P, Q_TILES, N], F32, name="logged")
-        result = keep.tile([P, Q_TILES, N], F32, name="result")
+        result = keep.tile([P, Q_TILES, N], F32, name="result", align_bytes=256)
         for m in range(Q_TILES):
             for c in range(N_TILES):
                 cols = slice(c * P, (c + 1) * P)

@@ -1,7 +1,6 @@
 from contextlib import ExitStack
 
 import concourse.mybir as mybir
-from concourse.masks import make_identity
 
 N, T, D, NQ = 512, 2048, 1024, 256
 FLOPS = 2 * D * NQ * N
@@ -28,9 +27,10 @@ HALF_TILES = HALF // P
 LIST_ROWS = 16
 HALF_COLS = HALF // LIST_ROWS
 SCALE_ROWS = 4
-PASS_SHIFT = 16
-SHIFT_RUNS = ((0, 64), (64, 96), (96, 112))
-EARLY = 512
+QUAD = 32
+QUADS = P // QUAD
+STAGE = P - QUAD
+ROW_ALIGN = 256
 PIECE = 1024
 SHARE = (64, 96)
 RUN = 2
@@ -43,6 +43,7 @@ def tile_attend_bpr_topk_kernel(tc, qT, k_words, k_scales, ib, ps, offs, out):
     with ExitStack() as ctx:
         keep = ctx.enter_context(tc.tile_pool(name="keep", bufs=1))
         reuse = ctx.enter_context(tc.tile_pool(name="reuse", bufs=1))
+        late = ctx.enter_context(tc.tile_pool(name="late", bufs=1))
         psum = ctx.enter_context(tc.psum_pool(name="psum", bufs=1))
 
         def list_half(h):
@@ -50,69 +51,75 @@ def tile_attend_bpr_topk_kernel(tc, qT, k_words, k_scales, ib, ps, offs, out):
 
         offsets = keep.tile([P, N // LIST_ROWS], U16, name="offsets")
         nc.sync.dma_start(offsets[:], offs)
-        bias_pool = keep.tile([P, T], F32, name="bias_pool", align_bytes=256)
+        scale_pool = late.tile([P, T], U8, name="scale_pool", align_bytes=ROW_ALIGN, offset=0)
+        nc.sync.dma_start(
+            out=scale_pool[STAGE:P, :].bitcast(I32), in_=k_scales.bitcast(I32).rearrange("o f t -> (o f) t")
+        )
+        bias_pool = keep.tile([P, T], F32, name="bias_pool", align_bytes=ROW_ALIGN)
         nc.scalar.dma_start(out=bias_pool[P - 1 : P, :], in_=ib[0:1, :])
-
-        word_pool = keep.tile([P, T], U32, name="word_pool", align_bytes=256)
-        word_rows = k_words[0].rearrange("p t b -> p (t b)").bitcast(I32)
-        nc.sync.dma_start(out=word_pool[:, :EARLY].bitcast(I32), in_=word_rows[:, :EARLY])
-
-        scale_pool = keep.tile([P, T], U8, name="scale_pool", tag="scales", align_bytes=256)
-        nc.vector.memset(scale_pool[:].bitcast(I32), 0)
-        scale_rows = k_scales.bitcast(I32).rearrange("o (quad r) t -> r quad o t", r=SCALE_ROWS)
-        for r in range(SCALE_ROWS):
-            nc.sync.dma_start(out=scale_pool[r:P:PASS_SHIFT, :].bitcast(I32), in_=scale_rows[r])
+        word_pool = keep.tile([P, T], U32, name="word_pool", align_bytes=ROW_ALIGN)
+        nc.sync.dma_start(out=word_pool[:].bitcast(I32), in_=k_words[0].rearrange("p t b -> p (t b)").bitcast(I32))
+        q_rows = qT[0].rearrange("(o p j) n -> o p j n", p=P, j=PACK)
+        q_first = reuse.tile([P, PACK, NQ], F32, name="q_first", align_bytes=ROW_ALIGN, offset=3 * PIECE)
+        nc.sync.dma_start(out=q_first[:], in_=q_rows[0])
+        nc.vector.memset(scale_pool[0:STAGE, :].bitcast(I32), 0)
         nc.vector.memset(bias_pool[0 : P - 1, :], 0.0)
 
-        q_raw = [
-            reuse.tile([P, PACK, NQ], F32, name="q_raw0", align_bytes=256, offset=3 * PIECE),
-            keep.tile([P, PACK, NQ], F32, name="q_raw1", align_bytes=256),
-        ]
-        q_rows = qT[0].rearrange("(o p j) n -> o p j n", p=P, j=PACK)
-        nc.sync.dma_start(out=word_pool[:, EARLY:].bitcast(I32), in_=word_rows[:, EARLY:])
-        for o in range(PASSES):
-            nc.sync.dma_start(out=q_raw[o][:], in_=q_rows[o])
-
         ident = keep.tile([P, P], F32, name="ident", align_bytes=64)
-        nc.vector.memset(ident[:], 0.0)
-        make_identity(nc, ident[:], nomemset=True)
-        scale1 = keep.tile([P, N], U8, name="scale1", align_bytes=64)
-        nc.vector.memset(scale1[:].bitcast(I32), 0)
+        off_diagonal = keep.tile([P, P], F32, name="off_diagonal", align_bytes=64)
+        distance = late.tile([P, P], F32, name="distance", align_bytes=64, offset=6 * PIECE)[:]
+        nc.gpsimd.iota(off_diagonal[:], [[1, P]], base=0, channel_multiplier=-1, allow_small_or_imprecise_dtypes=True)
+        nc.scalar.activation(out=distance, in_=off_diagonal[:], func=ACT.Abs)
+        nc.scalar.activation(out=ident[:], in_=distance, func=ACT.Relu, scale=-1.0, bias=1.0)
+
+        picked_scales = keep.tile([P, N], U8, name="picked_scales", align_bytes=64)
+        nc.vector.tensor_copy(picked_scales[:], scale_pool[:].indirect(offsets[:]))
+        k_scale = [
+            late.tile([P, N], U8, name="k_scale%d" % o, align_bytes=ROW_ALIGN, offset=o * N) for o in range(PASSES)
+        ]
+
+        def place(o, quad):
+            src = STAGE + (o * QUADS + quad) * SCALE_ROWS
+            nc.sync.dma_start(
+                out=k_scale[o][quad * QUAD : quad * QUAD + SCALE_ROWS, :].bitcast(I32),
+                in_=picked_scales[src : src + SCALE_ROWS, :].bitcast(I32),
+            )
+
+        for quad in range(1, QUADS):
+            place(0, quad)
+        q_second = late.tile([P, PACK, NQ], F32, name="q_second", align_bytes=ROW_ALIGN, offset=3 * N)
+        nc.sync.dma_start(out=q_second[:], in_=q_rows[1])
+        pos = late.tile([P, Q_TILES], F32, name="pos", align_bytes=ROW_ALIGN, offset=2 * N)
+        with nc.allow_non_contiguous_dma(reason="one positive score a partition and query tile"):
+            nc.sync.dma_start(out=pos[:], in_=ps[0].rearrange("(m p) one -> p (m one)", p=P))
+        for quad in range(QUADS):
+            place(1, quad)
+        q_raw = [q_first, q_second]
 
         bias = keep.tile([P, N], F32, name="bias", align_bytes=64)
-        picked = [keep.tile([P, HALF], F32, name="picked%d" % h, align_bytes=64) for h in range(HALVES)]
+        picked = [
+            late.tile([P, HALF], F32, name="picked0", align_bytes=64, offset=6 * PIECE)[:],
+            reuse.tile([P, 3 * PIECE // 4], F32, name="picked1", align_bytes=64, offset=0)[:, :HALF],
+        ]
         turned = [
-            psum.tile([P, HALF_TILES, P], F32, name="turned%d" % h, tag="bank%d" % (N_TILES + h))
+            psum.tile([P, HALF_TILES, P], F32, name="turned%d" % h, tag="bank%d" % N_TILES)
             for h in range(HALVES)
         ]
         spread = [
             psum.tile([P, HALF_TILES, P], F32, name="spread%d" % h, tag="bank%d" % (N_TILES + HALVES + h))
             for h in range(HALVES)
         ]
-        columns = [
-            keep.tile([P, HALF_TILES], F32, name="columns0", align_bytes=64)[:],
-            reuse.tile([P, 3 * PIECE // 4], F32, name="columns1", align_bytes=64, offset=0)[:, :HALF_TILES],
-        ]
+        columns = [keep.tile([P, HALF_TILES], F32, name="columns%d" % h, align_bytes=64) for h in range(HALVES)]
+        nc.scalar.activation(out=picked[0], in_=bias_pool[:].indirect(list_half(0)), func=ACT.Copy)
+        nc.vector.tensor_copy(picked[1], bias_pool[:].indirect(list_half(1)))
+        nc.vector.tensor_copy(k_scale[0][0:QUAD, :].bitcast(I32), picked_scales[STAGE:P, :].bitcast(I32))
         for h in range(HALVES):
-            nc.vector.tensor_copy(picked[h][:], bias_pool[:].indirect(list_half(h)))
             for c in range(HALF_TILES):
                 nc.tensor.transpose(turned[h][:, c, :], picked[h][:, c * P : (c + 1) * P], ident[:])
-            nc.scalar.copy(out=columns[h], in_=turned[h][:, :, P - 1])
-        for h in range(HALVES):
+            nc.scalar.copy(out=columns[h][:], in_=turned[h][:, :, P - 1])
             for c in range(HALF_TILES):
                 nc.tensor.transpose(spread[h][:, c, :], columns[h][:, c : c + 1].to_broadcast([P, P]), ident[:])
-            nc.scalar.copy(out=bias[:, h * HALF : (h + 1) * HALF], in_=spread[h][:].rearrange("p c n -> p (c n)"))
-
-        scale0 = keep.tile([P, N], U8, name="scale0", align_bytes=64)
-        nc.vector.tensor_copy(scale0[:], scale_pool[:].indirect(offsets[:]))
-        for lo, hi in SHIFT_RUNS:
-            nc.sync.dma_start(
-                out=scale1[lo:hi, :].bitcast(I32), in_=scale0[lo + PASS_SHIFT : hi + PASS_SHIFT, :].bitcast(I32)
-            )
-        pos = keep.tile([P, Q_TILES], F32, name="pos", tag="scales", align_bytes=256)
-        with nc.allow_non_contiguous_dma(reason="one positive score a partition and query tile"):
-            nc.sync.dma_start(out=pos[:], in_=ps[0].rearrange("(m p) one -> p (m one)", p=P))
-        k_scale = [scale0, scale1]
+        nc.scalar.copy(out=bias[:, :HALF], in_=spread[0][:].rearrange("p c n -> p (c n)"))
 
         word_pairs = keep.tile([P, N], U32, name="word_pairs", align_bytes=64)
         by_pass = word_pairs[:].bitcast(U16).rearrange("p (n o) -> p o n", o=PASSES)
@@ -143,6 +150,7 @@ def tile_attend_bpr_topk_kernel(tc, qT, k_words, k_scales, ib, ps, offs, out):
         interleave(nc.scalar.copy, 0, 0, SHARE[0], P)
         nc.vector.tensor_copy(k_first[:].bitcast(U16), by_pass[:, 0, :])
         quantise(0, 0)
+        nc.vector.tensor_copy(bias[:, HALF:], spread[1][:].rearrange("p c n -> p (c n)"))
         interleave(nc.scalar.copy, 0, 1, 0, P)
         quantise(0, 1)
         k_second = reuse.tile([P, 2 * N], U8, name="k_second", align_bytes=64, offset=3 * PIECE)

@@ -66,11 +66,9 @@ def tile_attend_bpr_topk_kernel(tc, qT, k_words, k_scales, ib, ps, offs, out):
         nc.vector.memset(bias_pool[0 : P - 1, :], 0.0)
 
         ident = keep.tile([P, P], F32, name="ident", align_bytes=64)
-        off_diagonal = keep.tile([P, P], F32, name="off_diagonal", align_bytes=64)
-        distance = late.tile([P, P], F32, name="distance", align_bytes=64, offset=6 * PIECE)[:]
-        nc.gpsimd.iota(off_diagonal[:], [[1, P]], base=0, channel_multiplier=-1, allow_small_or_imprecise_dtypes=True)
-        nc.scalar.activation(out=distance, in_=off_diagonal[:], func=ACT.Abs)
-        nc.scalar.activation(out=ident[:], in_=distance, func=ACT.Relu, scale=-1.0, bias=1.0)
+        distance = late.tile([P, P], I32, name="distance", align_bytes=64, offset=6 * PIECE)
+        nc.gpsimd.iota(distance[:], [[1, P]], base=0, channel_multiplier=-1)
+        nc.scalar.activation(out=ident[:], in_=distance[:].bitcast(U32), func=ACT.Relu, scale=-1.0, bias=1.0)
 
         picked_scales = keep.tile([P, N], U8, name="picked_scales", align_bytes=64)
         nc.vector.tensor_copy(picked_scales[:], scale_pool[:].indirect(offsets[:]))
@@ -89,11 +87,11 @@ def tile_attend_bpr_topk_kernel(tc, qT, k_words, k_scales, ib, ps, offs, out):
             place(0, quad)
         q_second = late.tile([P, PACK, NQ], F32, name="q_second", align_bytes=ROW_ALIGN, offset=3 * N)
         nc.sync.dma_start(out=q_second[:], in_=q_rows[1])
+        for quad in range(QUADS):
+            place(1, quad)
         pos = late.tile([P, Q_TILES], F32, name="pos", align_bytes=ROW_ALIGN, offset=2 * N)
         with nc.allow_non_contiguous_dma(reason="one positive score a partition and query tile"):
             nc.sync.dma_start(out=pos[:], in_=ps[0].rearrange("(m p) one -> p (m one)", p=P))
-        for quad in range(QUADS):
-            place(1, quad)
         q_raw = [q_first, q_second]
 
         bias = keep.tile([P, N], F32, name="bias", align_bytes=64)

@@ -29,7 +29,6 @@ HALF_COLS = HALF // LIST_ROWS
 SCALE_ROWS = 4
 QUAD = 32
 QUADS = P // QUAD
-STAGE = P - QUAD
 ROW_ALIGN = 256
 PIECE = 1024
 SHARE = (64, 96)
@@ -53,7 +52,7 @@ def tile_attend_bpr_topk_kernel(tc, qT, k_words, k_scales, ib, ps, offs, out):
         nc.sync.dma_start(offsets[:], offs)
         scale_pool = late.tile([P, T], U8, name="scale_pool", align_bytes=ROW_ALIGN, offset=0)
         nc.sync.dma_start(
-            out=scale_pool[STAGE:P, :].bitcast(I32), in_=k_scales.bitcast(I32).rearrange("o f t -> (o f) t")
+            out=scale_pool[0:QUAD, :].bitcast(I32), in_=k_scales.bitcast(I32).rearrange("o f t -> (o f) t")
         )
         bias_pool = keep.tile([P, T], F32, name="bias_pool", align_bytes=ROW_ALIGN)
         nc.scalar.dma_start(out=bias_pool[P - 1 : P, :], in_=ib[0:1, :])
@@ -62,7 +61,8 @@ def tile_attend_bpr_topk_kernel(tc, qT, k_words, k_scales, ib, ps, offs, out):
         q_rows = qT[0].rearrange("(o p j) n -> o p j n", p=P, j=PACK)
         q_first = reuse.tile([P, PACK, NQ], F32, name="q_first", align_bytes=ROW_ALIGN, offset=3 * PIECE)
         nc.sync.dma_start(out=q_first[:], in_=q_rows[0])
-        nc.vector.memset(scale_pool[0:STAGE, :].bitcast(I32), 0)
+        nc.vector.memset(scale_pool[QUAD : 2 * QUAD, :].bitcast(I32), 0)
+        nc.vector.memset(scale_pool[2 * QUAD : P, :].bitcast(I32), 0)
         nc.vector.memset(bias_pool[0 : P - 1, :], 0.0)
 
         ident = keep.tile([P, P], F32, name="ident", align_bytes=64)
@@ -77,7 +77,7 @@ def tile_attend_bpr_topk_kernel(tc, qT, k_words, k_scales, ib, ps, offs, out):
         ]
 
         def place(o, quad):
-            src = STAGE + (o * QUADS + quad) * SCALE_ROWS
+            src = (o * QUADS + quad) * SCALE_ROWS
             nc.sync.dma_start(
                 out=k_scale[o][quad * QUAD : quad * QUAD + SCALE_ROWS, :].bitcast(I32),
                 in_=picked_scales[src : src + SCALE_ROWS, :].bitcast(I32),
@@ -110,7 +110,7 @@ def tile_attend_bpr_topk_kernel(tc, qT, k_words, k_scales, ib, ps, offs, out):
         columns = [keep.tile([P, HALF_TILES], F32, name="columns%d" % h, align_bytes=64) for h in range(HALVES)]
         nc.scalar.activation(out=picked[0], in_=bias_pool[:].indirect(list_half(0)), func=ACT.Copy)
         nc.vector.tensor_copy(picked[1], bias_pool[:].indirect(list_half(1)))
-        nc.vector.tensor_copy(k_scale[0][0:QUAD, :].bitcast(I32), picked_scales[STAGE:P, :].bitcast(I32))
+        nc.vector.tensor_copy(k_scale[0][0:QUAD, :].bitcast(I32), picked_scales[0:QUAD, :].bitcast(I32))
         for h in range(HALVES):
             for c in range(HALF_TILES):
                 nc.tensor.transpose(turned[h][:, c, :], picked[h][:, c * P : (c + 1) * P], ident[:])

@@ -30,6 +30,7 @@ SCALE_ROWS = 4
 QUAD = 32
 QUADS = P // QUAD
 ROW_ALIGN = 256
+AHEAD = 2
 PIECE = 1024
 SHARE = (64, 96)
 RUN = 2
@@ -50,7 +51,7 @@ def tile_attend_bpr_topk_kernel(tc, qT, k_words, k_scales, ib, ps, offs, out):
 
         offsets = keep.tile([P, N // LIST_ROWS], U16, name="offsets")
         nc.sync.dma_start(offsets[:], offs)
-        scale_pool = late.tile([P, T], U8, name="scale_pool", align_bytes=ROW_ALIGN, offset=0)
+        scale_pool = late.tile([P, T], U8, name="scale_pool", align_bytes=ROW_ALIGN, offset=4 * PIECE)
         nc.sync.dma_start(
             out=scale_pool[0:QUAD, :].bitcast(I32), in_=k_scales.bitcast(I32).rearrange("o f t -> (o f) t")
         )
@@ -61,6 +62,11 @@ def tile_attend_bpr_topk_kernel(tc, qT, k_words, k_scales, ib, ps, offs, out):
         q_rows = qT[0].rearrange("(o p j) n -> o p j n", p=P, j=PACK)
         q_first = reuse.tile([P, PACK, NQ], F32, name="q_first", align_bytes=ROW_ALIGN, offset=3 * PIECE)
         nc.sync.dma_start(out=q_first[:], in_=q_rows[0])
+        pos = keep.tile([P, Q_TILES], F32, name="pos")
+        with nc.allow_non_contiguous_dma(reason="one positive score a partition and query tile"):
+            nc.sync.dma_start(out=pos[:], in_=ps[0].rearrange("(m p) one -> p (m one)", p=P))
+        q_second = late.tile([P, PACK, NQ], F32, name="q_second", align_bytes=ROW_ALIGN, offset=N)
+        nc.sync.dma_start(out=q_second[:, :AHEAD], in_=q_rows[1][:, :AHEAD])
         nc.vector.memset(scale_pool[QUAD : 2 * QUAD, :].bitcast(I32), 0)
         nc.vector.memset(scale_pool[2 * QUAD : P, :].bitcast(I32), 0)
         nc.vector.memset(bias_pool[0 : P - 1, :], 0.0)
@@ -73,7 +79,7 @@ def tile_attend_bpr_topk_kernel(tc, qT, k_words, k_scales, ib, ps, offs, out):
         picked_scales = keep.tile([P, N], U8, name="picked_scales", align_bytes=64)
         nc.vector.tensor_copy(picked_scales[:], scale_pool[:].indirect(offsets[:]))
         k_scale = [
-            late.tile([P, N], U8, name="k_scale%d" % o, align_bytes=ROW_ALIGN, offset=o * N) for o in range(PASSES)
+            late.tile([P, N], U8, name="k_scale%d" % o, align_bytes=ROW_ALIGN, offset=4 * PIECE + (1 + o) * N) for o in range(PASSES)
         ]
 
         def place(o, quad):
@@ -85,13 +91,9 @@ def tile_attend_bpr_topk_kernel(tc, qT, k_words, k_scales, ib, ps, offs, out):
 
         for quad in range(1, QUADS):
             place(0, quad)
-        q_second = late.tile([P, PACK, NQ], F32, name="q_second", align_bytes=ROW_ALIGN, offset=3 * N)
-        nc.sync.dma_start(out=q_second[:], in_=q_rows[1])
+        nc.sync.dma_start(out=q_second[:, AHEAD:], in_=q_rows[1][:, AHEAD:])
         for quad in range(QUADS):
             place(1, quad)
-        pos = late.tile([P, Q_TILES], F32, name="pos", align_bytes=ROW_ALIGN, offset=2 * N)
-        with nc.allow_non_contiguous_dma(reason="one positive score a partition and query tile"):
-            nc.sync.dma_start(out=pos[:], in_=ps[0].rearrange("(m p) one -> p (m one)", p=P))
         q_raw = [q_first, q_second]
 
         bias = keep.tile([P, N], F32, name="bias", align_bytes=64)

@@ -25,7 +25,6 @@ HALVES = 2
 HALF = N // HALVES
 HALF_TILES = HALF // P
 LIST_ROWS = 16
-HALF_COLS = HALF // LIST_ROWS
 SCALE_ROWS = 4
 QUAD = 32
 QUADS = P // QUAD
@@ -46,8 +45,8 @@ def tile_attend_bpr_topk_kernel(tc, qT, k_words, k_scales, ib, ps, offs, out):
         late = ctx.enter_context(tc.tile_pool(name="late", bufs=1))
         psum = ctx.enter_context(tc.psum_pool(name="psum", bufs=1))
 
-        def list_half(h):
-            return offsets[:, h * HALF_COLS : (h + 1) * HALF_COLS]
+        def listed(first, count):
+            return offsets[:, first // LIST_ROWS : (first + count) // LIST_ROWS]
 
         offsets = keep.tile([P, N // LIST_ROWS], U16, name="offsets")
         nc.sync.dma_start(offsets[:], offs)
@@ -97,10 +96,9 @@ def tile_attend_bpr_topk_kernel(tc, qT, k_words, k_scales, ib, ps, offs, out):
         q_raw = [q_first, q_second]
 
         bias = keep.tile([P, N], F32, name="bias", align_bytes=64)
-        picked = [
-            late.tile([P, HALF], F32, name="picked0", align_bytes=64, offset=6 * PIECE)[:],
-            reuse.tile([P, 3 * PIECE // 4], F32, name="picked1", align_bytes=64, offset=0)[:, :HALF],
-        ]
+        picked_first = late.tile([P, N - P], F32, name="picked_first", align_bytes=64, offset=6 * PIECE)
+        picked_last = reuse.tile([P, 3 * PIECE // 4], F32, name="picked_last", align_bytes=64, offset=0)
+        picked = [picked_first[:, c * P : (c + 1) * P] for c in range(N_TILES - 1)] + [picked_last[:, :P]]
         turned = [
             psum.tile([P, HALF_TILES, P], F32, name="turned%d" % h, tag="bank%d" % N_TILES)
             for h in range(HALVES)
@@ -110,12 +108,13 @@ def tile_attend_bpr_topk_kernel(tc, qT, k_words, k_scales, ib, ps, offs, out):
             for h in range(HALVES)
         ]
         columns = [keep.tile([P, HALF_TILES], F32, name="columns%d" % h, align_bytes=64) for h in range(HALVES)]
-        nc.scalar.activation(out=picked[0], in_=bias_pool[:].indirect(list_half(0)), func=ACT.Copy)
-        nc.vector.tensor_copy(picked[1], bias_pool[:].indirect(list_half(1)))
+        nc.scalar.activation(out=picked_first[:, :HALF], in_=bias_pool[:].indirect(listed(0, HALF)), func=ACT.Copy)
+        nc.scalar.activation(out=picked[2], in_=bias_pool[:].indirect(listed(HALF, P)), func=ACT.Copy)
+        nc.vector.tensor_copy(picked[3], bias_pool[:].indirect(listed(N - P, P)))
         nc.vector.tensor_copy(k_scale[0][0:QUAD, :].bitcast(I32), picked_scales[0:QUAD, :].bitcast(I32))
         for h in range(HALVES):
             for c in range(HALF_TILES):
-                nc.tensor.transpose(turned[h][:, c, :], picked[h][:, c * P : (c + 1) * P], ident[:])
+                nc.tensor.transpose(turned[h][:, c, :], picked[h * HALF_TILES + c], ident[:])
             nc.scalar.copy(out=columns[h][:], in_=turned[h][:, :, P - 1])
             for c in range(HALF_TILES):
                 nc.tensor.transpose(spread[h][:, c, :], columns[h][:, c : c + 1].to_broadcast([P, P]), ident[:])

from contextlib import ExitStack

import concourse.mybir as mybir

N, T, D, NQ = 512, 2048, 1024, 256
FLOPS = 2 * D * NQ * N

F32 = mybir.dt.float32
BF16 = mybir.dt.bfloat16
I32 = mybir.dt.int32
U32 = mybir.dt.uint32
U16 = mybir.dt.uint16
U8 = mybir.dt.uint8
FP8X4 = mybir.dt.float8_e4m3fn_x4
FP4X4 = mybir.dt.float4_e2m1fn_x4
ALU = mybir.AluOpType
ACT = mybir.ActivationFunctionType

P = 128
PACK = 4
PASSES = D // (P * PACK)
Q_TILES = NQ // P
N_TILES = N // P
HALVES = 2
HALF = N // HALVES
HALF_TILES = HALF // P
LIST_ROWS = 16
SCALE_ROWS = 4
QUAD = 32
QUADS = P // QUAD
ROW_ALIGN = 256
AHEAD = 2
PIECE = 1024
SHARE = (64, 96)
RUN = 2
EXP_CAP = 2.0 ** 60
STORES = [(0, 0, 128), (0, 128, 384), (0, 384, 512), (1, 0, 256), (1, 256, 512)]


def tile_attend_bpr_topk_kernel(tc, qT, k_words, k_scales, ib, ps, offs, out):
    nc = tc.nc
    with ExitStack() as ctx:
        keep = ctx.enter_context(tc.tile_pool(name="keep", bufs=1))
        reuse = ctx.enter_context(tc.tile_pool(name="reuse", bufs=1))
        late = ctx.enter_context(tc.tile_pool(name="late", bufs=1))
        psum = ctx.enter_context(tc.psum_pool(name="psum", bufs=1))

        def listed(first, count):
            return offsets[:, first // LIST_ROWS : (first + count) // LIST_ROWS]

        offsets = keep.tile([P, N // LIST_ROWS], U16, name="offsets")
        nc.sync.dma_start(offsets[:], offs)
        scale_pool = late.tile([P, T], U8, name="scale_pool", align_bytes=ROW_ALIGN, offset=4 * PIECE)
        nc.sync.dma_start(
            out=scale_pool[0:QUAD, :].bitcast(I32), in_=k_scales.bitcast(I32).rearrange("o f t -> (o f) t")
        )
        bias_pool = keep.tile([P, T], F32, name="bias_pool", align_bytes=ROW_ALIGN)
        nc.scalar.dma_start(out=bias_pool[P - 1 : P, :], in_=ib[0:1, :])
        word_pool = keep.tile([P, T], U32, name="word_pool", align_bytes=ROW_ALIGN)
        nc.sync.dma_start(out=word_pool[:].bitcast(I32), in_=k_words[0].rearrange("p t b -> p (t b)").bitcast(I32))
        q_rows = qT[0].rearrange("(o p j) n -> o p j n", p=P, j=PACK)
        q_first = reuse.tile([P, PACK, NQ], F32, name="q_first", align_bytes=ROW_ALIGN, offset=3 * PIECE)
        nc.sync.dma_start(out=q_first[:], in_=q_rows[0])
        pos = keep.tile([P, Q_TILES], F32, name="pos")
        with nc.allow_non_contiguous_dma(reason="one positive score a partition and query tile"):
            nc.sync.dma_start(out=pos[:], in_=ps[0].rearrange("(m p) one -> p (m one)", p=P))
        q_second = late.tile([P, PACK, NQ], F32, name="q_second", align_bytes=ROW_ALIGN, offset=N)
        nc.sync.dma_start(out=q_second[:, :AHEAD], in_=q_rows[1][:, :AHEAD])
        nc.vector.memset(scale_pool[QUAD : 2 * QUAD, :].bitcast(I32), 0)
        nc.vector.memset(scale_pool[2 * QUAD : P, :].bitcast(I32), 0)
        nc.vector.memset(bias_pool[0 : P - 1, :], 0.0)

        ident = keep.tile([P, P], F32, name="ident", align_bytes=64)
        distance = late.tile([P, P], I32, name="distance", align_bytes=64, offset=6 * PIECE)
        nc.gpsimd.iota(distance[:], [[1, P]], base=0, channel_multiplier=-1)
        nc.scalar.activation(out=ident[:], in_=distance[:].bitcast(U32), func=ACT.Relu, scale=-1.0, bias=1.0)

        picked_scales = keep.tile([P, N], U8, name="picked_scales", align_bytes=64)
        nc.vector.tensor_copy(picked_scales[:], scale_pool[:].indirect(offsets[:]))
        k_scale = [
            late.tile([P, N], U8, name="k_scale%d" % o, align_bytes=ROW_ALIGN, offset=4 * PIECE + (1 + o) * N) for o in range(PASSES)
        ]

        def place(o, quad):
            src = (o * QUADS + quad) * SCALE_ROWS
            nc.sync.dma_start(
                out=k_scale[o][quad * QUAD : quad * QUAD + SCALE_ROWS, :].bitcast(I32),
                in_=picked_scales[src : src + SCALE_ROWS, :].bitcast(I32),
            )

        for quad in range(1, QUADS):
            place(0, quad)
        nc.sync.dma_start(out=q_second[:, AHEAD:], in_=q_rows[1][:, AHEAD:])
        for quad in range(QUADS):
            place(1, quad)
        q_raw = [q_first, q_second]

        bias = keep.tile([P, N], F32, name="bias", align_bytes=64)
        picked_first = late.tile([P, N - P], F32, name="picked_first", align_bytes=64, offset=6 * PIECE)
        picked_last = reuse.tile([P, 3 * PIECE // 4], F32, name="picked_last", align_bytes=64, offset=0)
        picked = [picked_first[:, c * P : (c + 1) * P] for c in range(N_TILES - 1)] + [picked_last[:, :P]]
        turned = [
            psum.tile([P, HALF_TILES, P], F32, name="turned%d" % h, tag="bank%d" % N_TILES)
            for h in range(HALVES)
        ]
        spread = [
            psum.tile([P, HALF_TILES, P], F32, name="spread%d" % h, tag="bank%d" % (N_TILES + HALVES + h))
            for h in range(HALVES)
        ]
        columns = [keep.tile([P, HALF_TILES], F32, name="columns%d" % h, align_bytes=64) for h in range(HALVES)]
        nc.scalar.activation(out=picked_first[:, :HALF], in_=bias_pool[:].indirect(listed(0, HALF)), func=ACT.Copy)
        nc.scalar.activation(out=picked[2], in_=bias_pool[:].indirect(listed(HALF, P)), func=ACT.Copy)
        nc.vector.tensor_copy(picked[3], bias_pool[:].indirect(listed(N - P, P)))
        nc.vector.tensor_copy(k_scale[0][0:QUAD, :].bitcast(I32), picked_scales[0:QUAD, :].bitcast(I32))
        for h in range(HALVES):
            for c in range(HALF_TILES):
                nc.tensor.transpose(turned[h][:, c, :], picked[h * HALF_TILES + c], ident[:])
            nc.scalar.copy(out=columns[h][:], in_=turned[h][:, :, P - 1])
            for c in range(HALF_TILES):
                nc.tensor.transpose(spread[h][:, c, :], columns[h][:, c : c + 1].to_broadcast([P, P]), ident[:])
        nc.scalar.copy(out=bias[:, :HALF], in_=spread[0][:].rearrange("p c n -> p (c n)"))

        word_pairs = keep.tile([P, N], U32, name="word_pairs", align_bytes=64)
        by_pass = word_pairs[:].bitcast(U16).rearrange("p (n o) -> p o n", o=PASSES)
        k_first = reuse.tile([P, 2 * N], U8, name="k_first", align_bytes=64, offset=2 * PIECE)
        q_code = keep.tile([P, PASSES, NQ], U32, name="q_code", align_bytes=64)
        q_scale = [keep.tile([P, NQ], U8, name="q_scale%d" % o, align_bytes=64) for o in range(PASSES)]
        grouped = [
            reuse.tile([P, P, PACK], BF16, name="grouped%d" % u, align_bytes=64, offset=u * PIECE)
            for u in range(Q_TILES)
        ]

        def interleave(copy, o, m, lo, hi):
            copy(
                out=grouped[o * Q_TILES + m][:, lo:hi].rearrange("p (c i) j -> p c j i", i=RUN),
                in_=q_raw[o][:, :, m * P + lo : m * P + hi].rearrange("p j (c i) -> p c j i", i=RUN),
            )

        def quantise(o, m):
            rows = slice(m * P, (m + 1) * P)
            nc.vector.quantize_mx(
                out=q_code[:, o, rows].bitcast(FP8X4),
                scales=q_scale[o][:, rows],
                in_=grouped[o * Q_TILES + m][:].rearrange("p n j -> p (n j)"),
            )

        nc.vector.tensor_copy(word_pairs[:], word_pool[:].indirect(offsets[:]))
        interleave(nc.vector.tensor_copy, 0, 0, 0, SHARE[0])
        interleave(nc.scalar.copy, 0, 0, SHARE[0], P)
        nc.vector.tensor_copy(k_first[:].bitcast(U16), by_pass[:, 0, :])
        quantise(0, 0)
        nc.vector.tensor_copy(bias[:, HALF:], spread[1][:].rearrange("p c n -> p (c n)"))
        interleave(nc.scalar.copy, 0, 1, 0, P)
        quantise(0, 1)
        k_second = reuse.tile([P, 2 * N], U8, name="k_second", align_bytes=64, offset=3 * PIECE)
        second = reuse.tile([P, Q_TILES, P, PACK], BF16, name="grouped_second", align_bytes=64, offset=4 * PIECE)
        grouped.extend(second[:, m] for m in range(Q_TILES))
        interleave(nc.vector.tensor_copy, 1, 0, 0, SHARE[1])
        nc.vector.tensor_copy(k_second[:].bitcast(U16), by_pass[:, 1, :])
        interleave(nc.scalar.copy, 1, 0, SHARE[1], P)
        interleave(nc.scalar.copy, 1, 1, 0, P)
        quantise(1, 0)
        quantise(1, 1)

        k_code = [k_first, k_second]
        acc = [psum.tile([P, P], F32, name="acc%d" % u, tag="bank%d" % u) for u in range(Q_TILES * N_TILES)]
        for o in range(PASSES):
            for m in range(Q_TILES):
                rows = slice(m * P, (m + 1) * P)
                for c in range(N_TILES):
                    nc.tensor.matmul_mx(
                        out=acc[m * N_TILES + c][:],
                        lhsT=q_code[:, o, rows].bitcast(FP8X4),
                        lhsT_scale=q_scale[o][:, rows],
                        rhs=k_code[o][:, 2 * c * P : 2 * (c + 1) * P].bitcast(FP4X4),
                        rhs_scale=k_scale[o][:, c * P : (c + 1) * P],
                        start=(o == 0),
                        stop=(o == PASSES - 1),
                    )

        logit = keep.tile([P, Q_TILES, N], F32, name="logit")
        grown = keep.tile([P, Q_TILES, N], F32, name="grown")
        capped = keep.tile([P, Q_TILES, N], F32, name="capped")
        logged = keep.tile([P, Q_TILES, N], F32, name="logged")
        result = keep.tile([P, Q_TILES, N], F32, name="result", align_bytes=256)
        for m in range(Q_TILES):
            for c in range(N_TILES):
                cols = slice(c * P, (c + 1) * P)
                nc.vector.scalar_tensor_tensor(
                    out=logit[:, m, cols], in0=acc[m * N_TILES + c][:], scalar=pos[:, m : m + 1], in1=bias[:, cols],
                    op0=ALU.subtract, op1=ALU.add,
                )
                nc.scalar.activation(out=grown[:, m, cols], in_=logit[:, m, cols], func=ACT.Exp)
        nc.vector.tensor_scalar_min(out=capped[:], in0=grown[:], scalar1=EXP_CAP)
        for m, lo, hi in STORES:
            for first in range(lo, hi, P):
                cols = slice(first, first + P)
                nc.scalar.activation(out=logged[:, m, cols], in_=capped[:, m, cols], func=ACT.Ln, bias=1.0)
                nc.vector.tensor_tensor(out=result[:, m, cols], in0=logged[:, m, cols], in1=logit[:, m, cols], op=ALU.max)
            nc.sync.dma_start(out=out[0, m * P : (m + 1) * P, lo:hi], in_=result[:, m, lo:hi])
